import numpy as np, ml_dtypes
CORES = [5,29,101,125,133,157,229,253]
N = 8
import mx_ref
BF = ml_dtypes.bfloat16
def gentries(a):
    return np.ascontiguousarray(a.reshape(8, 16, -1).transpose(0, 2, 1)).reshape(8, -1)
def gtable(e):
    e = np.asarray(e); return np.ascontiguousarray(e.reshape(8, -1, 16).transpose(0, 2, 1)).reshape(128, -1).astype(np.int32)
def gcols(t, e):
    v = np.concatenate([t.reshape(8, 16, -1, 4), np.zeros((8, 16, 1, 4), BF)], axis=2)
    return np.ascontiguousarray(np.stack([v[g][:, e[g]] for g in range(8)])).reshape(128, -1)
def cols(t, e):
    v = np.concatenate([t.reshape(128, -1, 4), np.zeros((128, 1, 4), BF)], axis=1)
    return np.ascontiguousarray(v[:, e]).reshape(128, -1)
def tile(rs):
    return np.stack(rs, axis=2).reshape(128, -1).astype(BF)
def pick(q, e):
    c = np.concatenate([q[0].reshape(128, -1, 4), np.zeros((128, 1, 4), np.uint8)], axis=1); s = np.concatenate([q[1], np.ones((16, 1), np.uint8)], axis=1)
    return (np.ascontiguousarray(c[:, e].reshape(128, -1)), np.ascontiguousarray(s[:, e]))
def join(*qs):
    return (np.concatenate([q[0] for q in qs], axis=1), np.concatenate([q[1] for q in qs], axis=1))
def put(q, e, v):
    c, s = q[0].reshape(128, -1, 4).copy(), q[1].copy(); c[:, e] = v[0].reshape(128, -1, 4); s[:, e] = v[1]
    return (c.reshape(128, -1), s)
def pk(c, s):
    return (np.ascontiguousarray(c), mx_ref.live(s))
def emit(q):
    return q[0], q[1]
def packed(v, rng):
    q = [mx_ref.quantize(np.ascontiguousarray(v[r])) for r in range(N)]
    return np.stack([a for a, b in q]), np.stack([mx_ref.plane(b, rng) for a, b in q])
def values_of_codes():
    e, c = np.zeros((128, 128, 4), np.float32), np.zeros((128, 2, 4), np.uint8)
    e[np.arange(128), np.arange(128), 0] = 1
    c[:127, :, 0] = np.arange(256).reshape(2, 128).T[:127]
    return mx_ref.matmul(mx_ref.quantize(e.reshape(128, 512).astype(BF)), (c.reshape(128, 8), np.full((16, 2), 127, np.uint8))).T.reshape(-1).astype(np.float64)
CODE_VALUE, SCALE_VALUE = values_of_codes(), 2.0 ** (np.arange(256) - 127.0)
def decode(q):
    return (CODE_VALUE[q[0]].reshape(16, 8, -1, 4) * SCALE_VALUE[q[1]][:, None, :, None] + 0.0).reshape(128, -1).astype(np.float32)
def f(rng, *shape):
    return mx_ref.flush((rng.standard_normal(shape, dtype=np.float32) * np.exp2(rng.integers(-2, 3, shape[:-1] + (1,)))).astype(BF))
def wide(rng, *shape, cols=0):
    v = rng.standard_normal(shape, dtype=np.float32) * np.exp2(rng.integers(-12, 13, shape)).astype(np.float32)
    if cols: v *= np.repeat(np.exp2(rng.integers(-cols, cols + 1, shape[:-2] + (1, shape[-1] // 4))) * (rng.random(shape[:-2] + (1, shape[-1] // 4)) > 0.0625), 4, axis=-1).astype(np.float32)
    return mx_ref.flush(v.astype(BF))
C, J, K, R = 256, 416, 96, 3
def big(v):
    v = v.astype(np.float32)
    v[np.abs(v) < np.float32(2.0 ** -16)] = 0
    return v.astype(BF)
def numbers_of(rng):
    return {"x": big(f(rng, N, 128, 4 * C)), "u": np.array(f(rng, N, 128, 512)), "v": np.array(f(rng, N, 128, 512))}
def paths(rng, n):
    a = np.zeros((8, J), np.int64)
    a[0] = rng.integers(0, C, J)
    for g in range(1, 8):
        a[g] = np.where(rng.random(J) < 0.5, a[g - 1], n[rng.integers(0, 8, J), a[g - 1]])
    return a
def lists(rng):
    n = rng.integers(0, C, (8, C))
    return {"nb": np.stack([gtable(n)] * N), "p": np.stack([gtable(paths(rng, n)) for r in range(N)])}
def weights(rng, kept=[]):
    w = (rng.random((N, 128, 512, 4), dtype=np.float32) * 2 - 1) * np.float32(2.0 ** -6)
    for i in range(2):
        k = rng.integers(0, 512, (N, 512))
        w[np.arange(N)[:, None], k >> 2, np.arange(512)[None], k & 3] = (3 + 6 * rng.random((N, 512))) * rng.choice([-1.0, 1.0], (N, 512))
    w = w.reshape(N, 128, 4, 128, 4)
    for i in kept:
        for h in range(i, 128, 16):
            w[:, :, :, h] = 0
            for b in range(4): w[:, h, b, h, b] = 32
    c, s = packed(w.reshape(N, 128, 2048).astype(BF), rng)
    return {"wc": c, "ws": s}
def setup_inputs(rng):
    return {**numbers_of(rng), **lists(rng), **weights(rng)}
def setup_inputs_ties(rng):
    d = numbers_of(rng)
    x = d["x"].reshape(N, 8, 16, C, 4)
    k = rng.integers(0, 3, (N, 8, C))
    k[:, rng.permutation(8)[:3]] = 1
    x[:, :, 0] = 0
    x[:, :, 0, :, 0] = k.astype(np.float32).astype(BF)
    z = (N, 8, 8, C, 4)
    odd = (1 + (2 * rng.integers(0, 64, z) + 1) * 2.0 ** -7) * np.exp2(-1.0 * rng.integers(8, 15, z)) * rng.choice([-1.0, 1.0], z)
    odd[:, :, 0, :, 0] = 1.96875
    o = rng.permutation(N)
    odd[o[2], :, 0, :, 1] = rng.integers(2, 32, (8, C)) * 2.0 ** -17
    x[:, :, 8:] = odd.astype(np.float32).astype(BF)
    u = d["u"].reshape(N, 128, 128, 4)
    u[:, :, ::16] = 0
    for r in range(N):
        for h in range(0, 128, 16):
            if r == o[2]: u[r, h + 8, h, 1] = 1.0
            else: u[r, h, h, 0] = 0.0 if r == o[0] else -1.0 if r == o[1] else 1.0
    l = lists(rng)
    t = np.array(gentries(l["p"][o[0]]))
    t[:, rng.permutation(J)[:J // 4]] = C - 32 + 4 * rng.integers(0, 8, (1, J // 4)) + np.arange(8)[:, None] % 2
    l["p"][o[0]] = gtable(t)
    return {"x": x.reshape(N, 128, 4 * C), "u": u.reshape(N, 128, 512), "v": d["v"], **l, **weights(rng, [0])}
def setup_inputs_near(rng):
    d = numbers_of(rng)
    x = d["x"].astype(np.float32).reshape(N, 8, 16, C, 4)
    x[:, :, :2] = 0
    x[:, :, 2:8] *= np.float32(0.25)
    x[:, :, 8:] = 0
    x[:, :, 0, :, 0] = 1
    x[:, :, 1, :, 0] = 2.0 ** -10
    s = rng.integers(0, 16, (N, 8, C))
    x[:, :, 8] = ((s[:, :, :, None] >> np.arange(4)) & 1) * np.exp2(np.arange(4) - 24.0)
    x[:, :, 10, :, 0] = (1 + 0.125 * rng.integers(0, 8, (N, 8, C))) * 2.0 ** -30
    x[:, :, 12] = x[:, :, 10]
    u = d["u"].reshape(N, 128, 128, 4)
    u[:, :, ::16] = 0
    o = rng.permutation(N) % 4
    for r in range(N):
        k = 2.0 ** -30 if o[r] in (1, 3) else 1.0
        sign = rng.permutation(8) % 2 * 2.0 - 1.0
        for g in range(8):
            h = 16 * g
            if o[r] == 3:
                u[r, h + 10, h, 0] = 1.125 * k * sign[g]
                u[r, h + 12, h, 0] = -k * sign[g]
            else:
                u[r, h, h, 0] = -k if o[r] == 2 else k
                u[r, h + 1, h, 0] = k
                u[r, h + 8, h] = 2 * k
    return {"x": x.reshape(N, 128, 4 * C).astype(BF), "u": u.reshape(N, 128, 512), "v": d["v"], **lists(rng), **weights(rng, [0, 1, 8, 9, 10, 11, 12, 13, 14, 15])}
def setup_inputs_huge(rng):
    d = numbers_of(rng)
    h = rng.permutation(8)
    x = -0.95 - 0.05 * rng.random((N, 8, 16, C, 4))
    x[:, h[4:]] = (0.75 + 0.1 * rng.random((N, 4, 16, C, 4))) * rng.choice([-1.0, 1.0], (N, 4, 1, C, 1))
    u = d["u"].reshape(N, 128, 128, 4)
    u[:, :, ::16] = 0
    for r in range(N):
        below = rng.permutation(8) < 4
        for g in range(8):
            a = 16 * int(rng.choice(h[:4] if below[g] else h[4:]))
            u[r, a:a + 16, 16 * g] = (2.0 ** 30 * (1 - 0.1 * rng.random((16, 4)))).astype(np.float32).astype(BF)
    return {"x": (2.0 ** 30 * x).astype(np.float32).reshape(N, 128, 4 * C).astype(BF), "u": u.reshape(N, 128, 512), "v": d["v"], **lists(rng), **weights(rng)}
def setup_inputs_ends(rng):
    d = numbers_of(rng)
    o = rng.permutation(N)
    sign = rng.integers(0, 2, (8, 16, 1, 4)) * 2.0 - 1.0
    x = np.zeros((N, 8, 16, C, 4))
    u = d["u"].reshape(N, 128, 128, 4)
    u[:, :, ::16] = 0
    v = np.zeros((N, 128, 512))
    n = rng.integers(0, C, (8, C))
    j = 1 + rng.permutation(C - 2)
    n[:, j[:C // 3]] = 0
    n[:, j[C // 3:2 * (C // 3)]] = C - 1
    t = np.stack([paths(rng, n) for r in range(N)])
    for i in range(N):
        r, k = o[i], 2.0 ** 30 if i % 2 == 0 else 2.0 ** -30
        if i % 2 == 0: x[r] = sign * k * (1 - 0.125 * rng.integers(0, 4, (8, 1, C, 1)))
        else: x[r] = sign * k * (1 + 0.125 * rng.integers(0, 8, (8, 1, C, 1)))
        none = 1 + rng.permutation(6)[:2]
        for g in range(8):
            if g in none: continue
            b = -1.0 if i == 0 else 1.0 if i == 2 else rng.choice([-1.0, 1.0])
            u[r, :, 16 * g] = (sign.reshape(128, 4) * (k * b)).astype(np.float32).astype(BF)
        v[r] = rng.choice([-1.0, 1.0], (128, 512)) * k
    t[o[0]] = C - 1
    t[o[1]] = 0
    t[o[2]] = np.where(np.arange(8) % 2 == 1, C - 1, 0)[:, None]
    return {"x": x.astype(np.float32).reshape(N, 128, 4 * C).astype(BF), "u": u.reshape(N, 128, 512), "v": v.astype(np.float32).astype(BF), "nb": np.stack([gtable(n)] * N), "p": np.stack([gtable(t[r]) for r in range(N)]), **weights(rng, range(16))}
def setup_inputs_spread(rng):
    d = setup_inputs(rng)
    d["x"] = big(wide(rng, N, 128, 4 * C, cols=6))
    return d
def check_inputs(d):
    b = []
    for k in ("x", "u", "v"):
        a = np.abs(d[k].astype(np.float32))
        if not (np.isfinite(a).all() and ((a == 0) | (a >= 2.0 ** -30) & (a <= 2.0 ** 30)).all()): b.append("a value of " + k)
    for k in ("nb", "p"):
        if not ((d[k] >= 0) & (d[k] < C)).all(): b.append("an entry of " + k)
    if (d["nb"] != d["nb"][:1]).any(): b.append("nb isn't the same on all ranks")
    none, least, most = [emit(mx_ref.quantize(np.full((128, 16), k, np.float32).astype(BF)))[1][0, 0] for k in (0.0, 2.0 ** -30, 2.0 ** 30)]
    tops = emit(mx_ref.quantize((np.ones((128, 1)) * np.repeat(1 + np.arange(128) * 2.0 ** -7, 4)).astype(np.float32).astype(BF)))[0] & 0x7F
    for r in range(N):
        if ((d["wc"][r] & 0x7F) == 0x7F).any(): b.append("wc: a code that is no number")
        s = mx_ref.live(d["ws"][r])
        if ((s != none) & ((s < least) | (s > most))).any(): b.append("ws: a scale out of range")
        elif not (np.sum(np.abs(decode(pk(d["wc"][r], d["ws"][r])).astype(np.float64)).reshape(128, 512, 4), axis=(0, 2)) <= 32).all(): b.append("the sizes in a column of W")
        a = np.max((d["wc"][r] & 0x7F).reshape(16, 8, 512, 4), axis=(1, 3))
        if not np.where(s == none, a == 0, (a >= np.min(tops)) & (a <= np.max(tops))).all(): b.append("wc: the codes of a block")
    return b
def hop(a, s, n):
    a = np.array(a)
    best = [n[np.argmax(s[e][n], axis=0), np.arange(C)] for e in (0, 7)]
    for h in range(4):
        for g in range(h % 2, 8, 2):
            if g == 0 or g == 7:
                m = a[1] if g == 0 else a[6]
                b = np.where(a[g] == m, best[0 if g == 0 else 1][m], m)
            else:
                low, high = a[g - 1] == a[g], a[g + 1] == a[g]
                b = np.where(low & ~high, a[g + 1], np.where(high & ~low, a[g - 1], a[g]))
            a[g] = np.where(s[g][b] > s[g][a[g]], b, a[g])
    return a
def reference(x, u, v, nb, p, wc, ws):
    qu = [mx_ref.quantize(u[r]) for r in range(N)]
    lay = [pk(wc[r], ws[r]) for r in range(N)]
    now = [x[r] for r in range(N)]
    at = [gentries(p[r]) for r in range(N)]
    for t in range(R):
        have, moved, z, first, gone = [], [], [], [], []
        for r in range(N):
            q = mx_ref.quantize(now[r])
            have.append(decode(q).astype(BF))
            s = mx_ref.matmul(qu[r], q)[::16] + np.float32(0.0)
            a = hop(at[r], s, gentries(nb[r]))
            bond = np.concatenate([a[1:], a[6:7]])
            z.append(((gcols(have[r], a).astype(np.float32) + gcols(have[r], bond).astype(np.float32)) * np.float32(0.5)).astype(BF))
            first.append(np.argsort(-np.sum(a[:-1] != a[1:], axis=0), kind="stable")[:K])
            gone.append(mx_ref.quantize(np.ascontiguousarray(cols(z[r], first[r]))))
            moved.append(a)
        for r in range(N):
            e = (r - 1) % N
            l = tile([mx_ref.matmul(pick(lay[r], np.arange(128 * b, 128 * b + 128)), gone[e]) * np.float32(0.03125) for b in range(4)])
            y = np.array(z[r]).reshape(128, J, 4)
            y[:, first[r]] = l.reshape(128, K, 4)
            at[r] = np.array(moved[r])
            at[r][:, first[r]] = moved[e][:, first[e]]
            low = np.stack([J + np.arange(C)] * 8)
            np.minimum.at(low, (np.arange(8)[:, None], at[r]), np.arange(J)[None])
            w = gcols(np.concatenate([y.reshape(128, 4 * J), have[r]], axis=1), low)
            now[r] = ((have[r].astype(np.float32) + w.astype(np.float32)) * np.float32(0.5)).astype(BF)
    y, ad = np.zeros((N, 128, C), np.float32), np.zeros((N, 8, J), np.float32)
    oc, osc = np.zeros((N, 128, 4 * C), np.uint8), np.zeros((N, 16, C), np.uint8)
    for r in range(N):
        q = mx_ref.quantize(now[r])
        y[r] = mx_ref.matmul(mx_ref.quantize(v[r]), q)
        ad[r] = at[r]
        oc[r], osc[r] = emit(q)
    return {"y": y, "ad": ad, "oc": oc, "osc": osc}

@@ -1,0 +1,580 @@
+from concourse.mybir import dt, AluOpType, AxisListType, ActivationFunctionType
+
+A = AluOpType
+AF = ActivationFunctionType
+C, J, K, R = 256, 416, 96, 3
+F32, BF, I32, U16, CODE, U8 = "float32", "bfloat16", "int32", "uint16", "float8_e4m3fn_x4", "uint8"
+BIGID, UNIT, LOW = 2.0 ** 80, 2.0 ** 72, 9.0e29
+SCRATCH, PLACE = {}, {}
+
+
+def _b(dtype, **sizes):
+    for k, n in sizes.items():
+        SCRATCH[k] = ("sbuf", [128, n], dtype)
+
+
+def _small(dtype, buf, **sizes):
+    at = 0
+    for k, n in sizes.items():
+        PLACE[k] = (buf, at)
+        at += (n + 31) // 32 * 32
+    SCRATCH[buf] = ("sbuf", [128, at], dtype)
+
+
+_b(BF, xt=1024, mt=1024, ut=512, vt=512, ones=512, eb=2048, fh=1024, fq=1024, fr=1024, fp=1024, hl=1408, at=512, tb=384)
+_b(CODE, qu=128, qv=128, uq=128, bq=128, qe=512, wq=512, qa=128)
+_b(U8, qus=128, qvs=128, uqs=128, bqs=128, qes=512, wqs=512, qas=128)
+for _t in range(R + 1):
+    _b(CODE, **{"qc%d" % _t: 256})
+    _b(U8, **{"qs%d" % _t: 256})
+for _t in range(R):
+    _b(CODE, **{"rc%d" % _t: 256, "fc%d" % _t: 256})
+    _b(U8, **{"rs%d" % _t: 256, "fs%d" % _t: 256})
+    _b(I32, **{"lo%d" % _t: 8, "rl%d" % _t: 8, "la%d" % _t: 8})
+_b(F32, ic=256, m16=256, enc=256, encs=256, cmax=256, fm=256, fm2=256, a1k=256, a17=256, b256=256, id1=4096,
+   tab=256, bt=256, jt=256, nbv=288, d1=128, ns=288, tw=512, ti=512, o0=576, o1=576, t0=576, t1=576, kr=416, plr=416,
+   dum=1248, cmp=416, ar=416, br=416, z2r=416, z1r=416, z2s=416, z1s=416, fa=256, fb=256, ab=1280, sbw=672, brr=256, aa=384,
+   zt=416, yo=256, ado=416)
+_small(F32, "pf", wcs=96, i96=96, cst=16, pl0=32, jb=32, fl0=64, fl1=64, sm=192, fi=64, eq=64, k4=16, low=16, lt=64, py=96, zy=96,
+       lw=16, lf=64)
+_b(I32, pi=16, s2=8, s8=8, nsi=8, kri=416)
+_small(I32, "qi", nbi=16, pin=32, cz=32, zc=32, ids=32, sw4=16, pl=4, ob=64, gb=64, iab=96, rk=4, gr=32, zi=96, pii=96, ia=16, lai=32)
+_b(U16, lu=8, lb=8)
+_small(U16, "pu", nbl=18, l0=40, l1=40, gk=32, lsa=32, lsb=32, lsp=32, lr=32, laa=8, lbb=8, lsl=16, lbl=16, lfl=16)
+SCRATCH["pa"] = ("psum", [128, 2048], F32)
+SCRATCH["pb"] = ("psum", [128, 2048], F32)
+DMAS = ["dX", "dU", "dW", "dV", "dN", "dP", "dJ", "dK", "dR", "dZ", "dO"]
+SEMAPHORES = ["sV", "sS", "sT", "sG", "snt"] + DMAS + [k + str(t) for t in range(R) for k in ("aC", "aS", "aL", "bC", "bS", "bL")]
+HALF = ((0, 13, 0, 208), (16, 29, 208, 416))
+
+
+def relays(topo, cores, r):
+    src, dst = cores[r], cores[(r + 1) % len(cores)]
+    ok = [c for c in topo.cores_of(src) if c not in cores and topo.may_write(c, dst)]
+    ok.sort(key=lambda c: (topo.die(c) != topo.die(src), c))
+    return ok[0], ok[1]
+
+
+def put(g, T, topo, core, dst, out, in_, sem):
+    rid, pid = topo.addr(dst, core)
+    g.remote_dma(out, in_, T.sem[sem], T.sem.snt, pid, rid, sum(1 << k for k in topo.engines(core, dst)[:8]))
+
+
+def relay_program(g, core, T, topo):
+    n, sent = len(T.cores), 0
+    for r in range(n):
+        a, b = relays(topo, T.cores, r)
+        dst = T.cores[(r + 1) % n]
+        for t in range(R):
+            if core == a:
+                g.wait_ge(T.sem["aC%d" % t], 8)
+                put(g, T, topo, core, dst, T["fc%d" % t][:, 0:C].bitcast(dt.uint8), T["rc%d" % t][:, 0:C].bitcast(dt.uint8), "bC%d" % t)
+                sent += 8
+            if core == b:
+                g.wait_ge(T.sem["aS%d" % t], 8)
+                put(g, T, topo, core, dst, T["fs%d" % t][:, 0:C], T["rs%d" % t][:, 0:C], "bS%d" % t)
+                g.wait_ge(T.sem["aL%d" % t], 8)
+                put(g, T, topo, core, dst, T["la%d" % t][:, 0:8], T["rl%d" % t][:, 0:8], "bL%d" % t)
+                sent += 16
+    if sent:
+        g.wait_ge(T.sem.snt, sent)
+
+
+def rank_program(g, core, T, topo):
+    rank = T.rank_of(core)
+    if rank is None:
+        relay_program(g, core, T, topo)
+        return
+    V, S, TE = g.vector, g.scalar, g.tensor
+    eng = {"V": V, "S": S, "T": TE, "G": g, "Y": g.sync}
+    total, known, recs = {}, {}, {}
+
+    def W(name, a, b, step=1, p0=0, p1=128, ps=1):
+        if name in PLACE:
+            name, o = PLACE[name]
+            a, b = a + o, b + o
+        t = T[name]
+        if (p0, p1, ps) == (0, 128, 1):
+            ap = t[:, a:b] if step == 1 else t[:, a:b:step]
+        else:
+            ap = t[p0:p1, a:b] if ps == 1 else t[p0:p1:ps, a:b]
+        if name in ("pa", "pb"):
+            a, b = a // 512 * 512, (b + 511) // 512 * 512
+        return {"ap": ap, "reg": (name, p0, p1, a, b, step, a % step), "aux": []}
+
+    def ind(win, lst):
+        return {"ap": win["ap"].indirect(lst["ap"]), "reg": win["reg"], "aux": [lst["reg"]]}
+
+    def u8(v):
+        return {"ap": v["ap"].bitcast(dt.uint8), "reg": v["reg"], "aux": []}
+
+    def u32(v):
+        return {"ap": v["ap"].bitcast(dt.uint32), "reg": v["reg"], "aux": []}
+
+    def ext(x):
+        return {"ap": x, "reg": None, "aux": []}
+
+    def meet(r, o):
+        if r[5] > 1 and r[5] == o[5] and r[6] != o[6]:
+            return False
+        return r[1] < o[2] and o[1] < r[2] and r[3] < o[4] and o[3] < r[4]
+
+    def op(q, fn, outs, ins, sem=None, val=None):
+        rd = [r for v in ins for r in [v["reg"]] + v["aux"] if r] + [r for v in outs for r in v["aux"]]
+        wr = [v["reg"] for v in outs if v["reg"]] + [r for r in rd if r[0] in ("pa", "pb")]
+        me = sem if sem else "s" + q
+        need = {}
+        for kind, regs in (("r", rd), ("w", wr)):
+            for r in regs:
+                for o, ok, os_, ov in recs.get(r[0], []):
+                    if not meet(r, o) or (kind == "r" and ok == "r"):
+                        continue
+                    if kind == "w" and ok == "w" and os_ == me and me in DMAS:
+                        continue
+                    need[os_] = max(need.get(os_, 0), total[os_] if os_ in DMAS else ov)
+        kn = known.setdefault(q, {})
+        for s in sorted(need):
+            if kn.get(s, 0) < need[s]:
+                eng[q].wait_ge(T.sem[s], need[s])
+                kn[s] = need[s]
+        c = fn()
+        amount = val if val else 16 if me in DMAS else 1
+        if val is None:
+            c.then_inc(T.sem[me], amount)
+        total[me] = total.get(me, 0) + amount
+        for kind, regs in (("r", rd), ("w", wr)):
+            for r in regs:
+                keep = []
+                for rec in recs.get(r[0], []):
+                    o = rec[0]
+                    inside = r[1] <= o[1] and o[2] <= r[2] and r[3] <= o[3] and o[4] <= r[4] and (r[5] == 1 or r[5:] == o[5:])
+                    if not (inside and (kind == "w" or (rec[1] == "r" and rec[2] == me))):
+                        keep.append(rec)
+                recs[r[0]] = keep + [(r, kind, me, total[me])]
+
+    def landed(name, n, sem):
+        recs.setdefault(name, []).append(((name, 0, 128, 0, n, 1, 0), "w", sem, 8))
+
+    def tt(out, a, b, o):
+        op("V", lambda: V.tensor_tensor(out["ap"], a["ap"], b["ap"], o), [out], [a, b])
+
+    def ts(out, a, s1, o1, s2=None, o2=None):
+        ins = [a] + [s for s in (s1, s2) if isinstance(s, dict)]
+        x1, x2 = [s["ap"] if isinstance(s, dict) else s for s in (s1, s2)]
+        if o2 is None:
+            op("V", lambda: V.tensor_scalar(out["ap"], a["ap"], x1, None, o1), [out], ins)
+        else:
+            op("V", lambda: V.tensor_scalar(out["ap"], a["ap"], x1, x2, o1, o2), [out], ins)
+
+    def cp(out, a):
+        op("V", lambda: V.tensor_copy(out["ap"], a["ap"]), [out], [a])
+
+    def fill(out, c):
+        op("V", lambda: V.memset(out["ap"], c), [out], [])
+
+    def red(out, a, o, size=False):
+        kw = {"apply_absolute_value": True} if size else {}
+        op("V", lambda: V.tensor_reduce(out["ap"], a["ap"], AxisListType.X, o, **kw), [out], [a])
+
+    def tr(out, a):
+        op("V", lambda: V.transpose(out["ap"], a["ap"]), [out], [a])
+
+    def quant(q, s, x):
+        op("V", lambda: V.quantize_mx(q["ap"], s["ap"], x["ap"]), [q, s], [x])
+
+    def act(out, a, f=AF.Copy, scale=None, bias=None, acc=None):
+        kw, ins, outs = {}, [a], [out]
+        if scale is not None:
+            kw["scale"] = scale
+        if bias is not None:
+            kw["bias"] = bias["ap"]
+            ins.append(bias)
+        if acc is not None:
+            kw["accum_out"] = acc["ap"]
+            outs.append(acc)
+        op("S", lambda: S.activation(out["ap"], a["ap"], f, **kw), outs, ins)
+
+    def mm(out, l, ls, r, rs):
+        op("T", lambda: TE.matmul_mx(out["ap"], l["ap"], ls["ap"], r["ap"], rs["ap"], True, True), [out], [l, ls, r, rs])
+
+    def dma(q, sem, out, in_):
+        op(q, lambda: eng[q].dma_start(out["ap"], in_["ap"]), [out], [in_], sem=sem)
+
+    def iota(out, pat, cm):
+        kw = {} if out["reg"][0] in ("pi", "s2", "s8") else {"allow_small_or_imprecise_dtypes": True}
+        op("G", lambda: g.iota(out["ap"], pat, 0, cm, **kw), [out], [])
+
+    def send(dst, out, src, sem):
+        op("G", lambda: put(g, T, topo, core, dst, out["ap"], src["ap"], sem), [], [src], sem="snt", val=8)
+
+    def fold(out, n_out, src, n, mask):
+        tt(W("fa", 0, n), src, W(mask, 0, n), A.mult)
+        a, b = "fa", "fb"
+        while n > n_out:
+            n //= 2
+            tt(out if n == n_out else W(b, 0, n), W(a, 0, 2 * n, 2), W(a, 1, 2 * n, 2), A.add)
+            a, b = b, a
+
+    def blk(p):
+        return p // 2 + 4 * (p % 2)
+
+    relA, relB = relays(topo, T.cores, rank)
+
+    dma("Y", "dX", W("xt", 0, 1024), ext(T.x[:, :]))
+    dma("S", "dU", W("ut", 0, 512), ext(T.u[:, :]))
+    for k in range(8):
+        t = (0, 4, 2, 6, 1, 5, 3, 7)[k]
+        dma("Y" if k % 2 else "S", "dN", W("nbi", 2 * k, 2 * k + 2), ext(T.nb[16 * t:16 * t + 16, :]))
+    fill(W("pin", 0, 32), 0)
+    for a in range(8):
+        q, h = a // 2, a % 2
+        dma("Y" if h else "S", "dP", W("pin", 16 * h, 16 * h + 13, 1, 32 * q, 32 * q + 32), ext(T.p[16 * a:16 * a + 16, :]))
+    dma("Y", "dW", u8(W("wq", 0, 512)), ext(T.wc[:, :]))
+    dma("Y", "dW", W("wqs", 0, 512), ext(T.ws[:, :]))
+    dma("Y", "dV", W("vt", 0, 512), ext(T.v[:, :]))
+
+    iota(W("pi", 0, 1), [[0, 1]], 1)
+    iota(W("s8", 0, 8), [[0, 8]], 1)
+    iota(W("s2", 0, 2), [[1, 2]], 2)
+    iota(W("ic", 0, 256), [[1, 256]], 0)
+    iota(W("encs", 0, 256), [[1, 16], [16, 16]], 0)
+    iota(W("pl0", 0, 32), [[0, 2], [16, 16]], 0)
+    fill(W("ones", 0, 512), 1.0)
+    for b in range(4):
+        o, i = W("eb", 512 * b, 512 * b + 512), W("ones", 0, 512)
+        op("G", lambda: g.affine_select(o["ap"], i["ap"], [[-1, 512]], A.is_equal, 0.0, b, 4), [o], [i])
+    iota(W("m16", 0, 256), [[0, 16], [1, 16]], 0)
+    iota(W("wcs", 0, 16), [[16, 16]], 0)
+    iota(W("i96", 0, 96), [[1, 96]], 0)
+    ts(W("s8", 0, 8), W("s8", 0, 8), 7, A.bitwise_and)
+    ts(W("lu", 0, 8), W("s8", 0, 8), 16, A.mult)
+    ts(W("nsi", 0, 8), W("s8", 0, 8), 1, A.bitwise_and)
+    ts(W("lb", 0, 8), W("nsi", 0, 8), 112, A.mult)
+    quant(W("qu", 0, 128), W("qus", 0, 128), W("ut", 0, 512))
+    for q, s, l in (("bq", "bqs", "lb"), ("uq", "uqs", "lu")):
+        cp(u32(W(q, 0, 128)), ind(u32(W("qu", 0, 128)), W(l, 0, 8)))
+        cp(W(s, 0, 128), ind(W("qus", 0, 128), W(l, 0, 8)))
+    quant(W("qc0", 0, 256), W("qs0", 0, 256), W("xt", 0, 1024))
+    ts(W("nsi", 0, 1), W("pi", 0, 1), 15, A.bitwise_and)
+    cp(W("cst", 0, 1), W("nsi", 0, 1))
+    lane = W("cst", 0, 1)
+    ts(W("cst", 1, 2), lane, 8, A.is_equal)
+    ts(W("cst", 2, 3), lane, 9, A.is_equal)
+    tt(W("cst", 3, 4), W("cst", 1, 2), W("cst", 2, 3), A.add)
+    ts(W("cst", 4, 5), W("cst", 3, 4), LOW, A.mult, LOW, A.subtract)
+    ts(W("enc", 0, 256), W("ic", 0, 256), UNIT, A.mult, BIGID, A.add)
+    ts(W("encs", 0, 256), W("encs", 0, 256), UNIT, A.mult, BIGID, A.add)
+    ts(W("cmax", 0, 256), W("enc", 0, 256), W("cst", 1, 2), A.mult, W("cst", 4, 5), A.add)
+    ts(W("encs", 0, 256), W("encs", 0, 256), W("cst", 2, 3), A.mult)
+    tt(W("cmax", 0, 256), W("cmax", 0, 256), W("encs", 0, 256), A.add)
+    ts(W("s2", 0, 2), W("s2", 0, 2), 15, A.bitwise_and)
+    ts(W("nsi", 2, 3), W("pi", 0, 1), 3, A.arith_shift_right)
+    cp(W("cst", 5, 6), W("nsi", 2, 3))
+    ts(W("nbl", 16, 18), W("s2", 0, 2), 16, A.mult, W("cst", 5, 6), A.add)
+    cp(W("nbl", 0, 16), W("nbi", 0, 16))
+    cp(W("nbv", 0, 288), ind(W("enc", 0, 256), W("nbl", 0, 18)))
+    tt(W("d1", 0, 128), W("nbv", 128, 256), W("nbv", 0, 128), A.subtract)
+    ts(W("nsi", 3, 4), W("pi", 0, 1), 1, A.bitwise_and)
+    ts(W("nsi", 4, 5), W("pi", 0, 1), 31, A.bitwise_and)
+    ts(W("nsi", 5, 6), W("nsi", 4, 5), 1, A.arith_shift_right)
+    ts(W("cst", 6, 7), W("nsi", 3, 4), 208, A.mult)
+    tt(W("cst", 7, 8), W("cst", 6, 7), W("nsi", 5, 6), A.add)
+    ts(W("pl0", 0, 32), W("pl0", 0, 32), W("cst", 7, 8), A.add)
+    ts(W("cz", 0, 32), W("pin", 0, 32), 1024, A.mult)
+    tt(W("cz", 0, 32), W("cz", 0, 32), W("pl0", 0, 32), A.add)
+
+    def to_chains():
+        for a in range(8):
+            q, h = a // 2, a % 2
+            dma("Y", "dZ", W("zc", 4 * blk(a), 4 * blk(a) + 4), W("cz", 16 * h, 16 * h + 16, 1, 32 * q, 32 * q + 32))
+    to_chains()
+    fill(W("jt", 0, 256), 0.0)
+    fill(W("fl0", 0, 64), 1.0)
+    fill(W("fl1", 0, 64), 1.0)
+    fill(W("at", 384, 512), 0.0)
+    for t in range(R):
+        fill(W("lo%d" % t, 0, 8), 0)
+    CW, CI, CWM, B10, B17 = [lambda k=0, n=16, o=o: W("wcs", o + k, o + k + n) for o in (0, 16, 32, 48, 64)]
+
+    def later_constants():
+        quant(W("qe", 0, 512), W("qes", 0, 512), W("eb", 0, 2048))
+        ts(W("fm", 0, 256), W("m16", 0, 256), lane, A.is_equal)
+        ts(W("a1k", 0, 256), W("ic", 0, 256), 1024.0, A.mult)
+        ts(W("fm2", 0, 256), W("fm", 0, 256), 2.0 ** -8, A.mult)
+        ts(W("b256", 0, 256), W("ic", 0, 256), 256.0, A.mult)
+        ts(CW(), CW(), lane, A.add)
+        ts(W("a17", 0, 256), W("ic", 0, 256), 2.0 ** 17, A.mult)
+        cp(W("sbw", 416, 672), W("b256", 0, 256))
+        ts(CI(), CW(), 416.0, A.add)
+        ts(CWM(), CW(), 256.0, A.subtract)
+        ts(B10(), CW(), -1024.0, A.mult)
+        ts(B17(), CW(), -2.0 ** 17, A.mult, 2.0 ** 24, A.add)
+        ts(W("i96", 0, 96), W("i96", 0, 96), 2.0 ** 24, A.subtract)
+        quant(W("qv", 0, 128), W("qvs", 0, 128), W("vt", 0, 512))
+
+    def code(out, x):
+        ts(out, x, 1 / UNIT, A.mult, 256.0, A.subtract)
+
+    def half_step(n):
+        tn, nt, no = "t%d" % (n % 2), "t%d" % ((n + 1) % 2), "o%d" % ((n + 1) % 2)
+        nx = "l%d" % ((n + 1) % 2)
+        par = (n - 1) % 2
+        fl = "fl%d" % par
+        ids = lambda b0, b1: W(tn, 64 * b0 + 8, 64 * b1, 16)
+        sc = lambda b, t: W(tn, 64 * b + t, 64 * b + 64, 16)
+        stay, move = 16 - 16 * par, 16 * par
+        if n < 4:
+            code(W(nx, stay, stay + 16), ids(4 - 4 * par, 8 - 4 * par))
+            pv = blk(7 - 7 * par)
+            code(W(nx, 32, 36), W(tn, 64 * pv + 9, 64 * pv + 64, 16))
+            act(W(no, 16 * stay, 16 * stay + 256), ind(W("tab", 0, 256), W(nx, stay, stay + 16)))
+            act(W(no, 512, 576), ind(W("jt", 0, 256), W(nx, 32, 36)))
+        else:
+            code(W("fi", 0, 16), ids(0, 4))
+        GL, GH, HI, LO = 0, 16, 32, 48
+        PW, DD, MM, SN, NI = [W("sm", o, o + k) for o, k in ((0, 32), (32, 32), (64, 32), (96, 16), (112, 16))]
+        D = lambda a, b: W("sm", 32 + a, 32 + b)
+        for i in range(4):
+            s, o = (2 * i, 4 + i) if par == 0 else (2 * i + 1, i)
+            f = (GH if par == 0 else GL) + 4 * i
+            tt(W(fl, f, f + 4), sc(o, s), sc(4 * par + i, s), A.is_gt)
+        for i in range(3):
+            s, o, m = (2 * i + 2, 4 + i, i + 1) if par == 0 else (2 * i + 1, i + 1, 4 + i)
+            f = GL + 4 * i + 4 if par == 0 else GH + 4 * i
+            tt(W(fl, f, f + 4), sc(o, s), sc(m, s), A.is_gt)
+        if par == 0:
+            tt(W(fl, HI, HI + 16), ids(0, 4), ids(4, 8), A.is_equal)
+            tt(W(fl, LO + 4, LO + 16), ids(1, 4), ids(4, 7), A.is_equal)
+            tt(D(16, 32), ids(4, 8), ids(0, 4), A.subtract)
+            tt(D(4, 16), ids(4, 7), ids(1, 4), A.subtract)
+            tt(PW, W(fl, 0, 32), W(fl, 32, 64), A.mult)
+            tt(D(0, 4), W(tn, 512, 576, 16), ids(0, 1), A.subtract)
+        else:
+            tt(W(fl, LO, LO + 16), ids(0, 4), ids(4, 8), A.is_equal)
+            tt(W(fl, HI, HI + 12), ids(4, 7), ids(1, 4), A.is_equal)
+            tt(D(0, 16), ids(0, 4), ids(4, 8), A.subtract)
+            tt(D(16, 28), ids(1, 4), ids(4, 7), A.subtract)
+            tt(PW, W(fl, 0, 32), W(fl, 32, 64), A.mult)
+            tt(D(28, 32), W(tn, 520, 576, 16), ids(7, 8), A.subtract)
+        tt(MM, PW, DD, A.mult)
+        tt(SN, W("sm", 64, 80), W("sm", 80, 96), A.add)
+        tt(NI, SN, ids(4 * par, 4 * par + 4), A.add)
+        if n == 4:
+            code(W("fi", 16, 32), NI)
+            return
+        code(W(nx, move, move + 16), NI)
+        hi, lo = 16 * move, 16 * stay
+        act(W(no, hi + 128, hi + 256), ind(W("tab", 0, 256), W(nx, move + 8, move + 16)))
+        cp(W(no, hi, hi + 128), ind(W("tab", 0, 256), W(nx, move, move + 8)))
+        tr(W(nt, lo, lo + 256), W(no, lo, lo + 256))
+        tr(W(nt, 512, 576), W(no, 512, 576))
+        tr(W(nt, hi, hi + 256), W(no, hi, hi + 256))
+
+    def next_chains():
+        tt(W("z1s", 0, 96), ind(W("a1k", 0, 256), W("laa", 0, 6)), W("pii", 0, 96), A.add)
+
+    for r in range(R):
+        q, s, lo, la = "qc%d" % r, "qs%d" % r, "lo%d" % r, "la%d" % r
+        if r:
+            quant(W(q, 0, 256), W(s, 0, 256), W("mt", 0, 1024))
+        send(relA, u8(W("rc%d" % r, 0, 256)), u8(W(q, 0, 256)), "aC%d" % r)
+        send(relB, W("rs%d" % r, 0, 256), W(s, 0, 256), "aS%d" % r)
+        if r == 0:
+            iota(W("id1", 0, 4096), [[1, 4096]], 0)
+        mq, ms = W(q, 0, 256), W(s, 0, 256)
+        mm(W("pb", 512, 768), W("bq", 0, 128), W("bqs", 0, 128), mq, ms)
+        mm(W("pb", 0, 256), W("uq", 0, 128), W("uqs", 0, 128), mq, ms)
+        if r:
+            next_chains()
+            tr(W("zt", 0, 416), W("z1s", 0, 416))
+            for h in range(2):
+                cp(W("cz", 16 * h, 16 * h + 13), W("zt", 16 * h, 416, 32))
+            to_chains()
+        act(W("bt", 0, 256), W("pb", 512, 768))
+        act(W("ns", 0, 288), ind(W("bt", 0, 256), W("nbl", 0, 18)))
+        tt(W("tab", 0, 256), W("pb", 0, 256), W("cmax", 0, 256), A.max)
+        tw, ti, ns = [lambda a, b, k=k: W(k, a, b) for k in ("tw", "ti", "ns")]
+        tt(tw(128, 256), ns(0, 128), ns(128, 256), A.max)
+        tt(tw(0, 128), ns(128, 256), ns(0, 128), A.is_gt)
+        tt(tw(320, 384), tw(128, 192), tw(192, 256), A.max)
+        tt(ti(0, 128), tw(0, 128), W("d1", 0, 128), A.mult)
+        tt(tw(256, 320), tw(192, 256), tw(128, 192), A.is_gt)
+        tt(ti(128, 256), ti(0, 128), W("nbv", 0, 128), A.add)
+        tt(tw(416, 448), tw(320, 352), tw(352, 384), A.max)
+        tt(ti(256, 320), ti(192, 256), ti(128, 192), A.subtract)
+        tt(tw(384, 416), tw(352, 384), tw(320, 352), A.is_gt)
+        tt(ti(320, 384), ti(256, 320), tw(256, 320), A.mult)
+        tt(tw(448, 480), tw(416, 448), ns(256, 288), A.is_gt)
+        tt(ti(384, 448), ti(320, 384), ti(128, 192), A.add)
+        tt(ti(448, 480), ti(416, 448), ti(384, 416), A.subtract)
+        tt(ti(480, 512), ti(448, 480), tw(384, 416), A.mult)
+        tt(ti(0, 32), ti(480, 512), ti(384, 416), A.add)
+        tt(ti(32, 64), ti(0, 32), W("nbv", 256, 288), A.subtract)
+        tt(ti(64, 96), ti(32, 64), tw(448, 480), A.mult)
+        tt(W("jb", 0, 32, 2), ti(64, 80), W("nbv", 256, 272), A.add)
+        tt(W("jb", 1, 32, 2), ti(80, 96), W("nbv", 272, 288), A.add)
+        for h in range(8):
+            dma("Y", "dJ", W("jt", 32 * h, 32 * h + 32, 1, 0, 128, 8), W("jb", 0, 32, 1, 16 * h, 16 * h + 16))
+        ts(W("ids", 0, 32), W("zc", 0, 32), 10, A.arith_shift_right)
+        cp(W("l1", 0, 32), W("ids", 0, 32))
+        act(W("o1", 256, 512), ind(W("tab", 0, 256), W("l1", 16, 32)))
+        cp(W("o1", 0, 256), ind(W("tab", 0, 256), W("l1", 0, 16)))
+        ts(W("sw4", 0, 4), W("ids", 0, 4), 15, A.bitwise_and)
+        ts(W("sw4", 8, 12), W("ids", 0, 4), 4, A.arith_shift_right)
+        ts(W("sw4", 4, 8), W("sw4", 0, 4), 16, A.mult)
+        tt(W("sw4", 12, 16), W("sw4", 4, 8), W("sw4", 8, 12), A.add)
+        cp(W("l1", 32, 36), W("sw4", 12, 16))
+        ts(W("pl", 0, 4), W("zc", 0, 4), 1023, A.bitwise_and)
+        tr(W("t1", 0, 256), W("o1", 0, 256))
+        tr(W("t1", 256, 512), W("o1", 256, 512))
+        if r == 0:
+            later_constants()
+        qe = lambda b: (W("qe", 128 * b, 128 * b + 128), W("qes", 128 * b, 128 * b + 128))
+        for b in range(4):
+            mm(W("pa", 512 * b, 512 * b + 256), qe(b)[0], qe(b)[1], mq, ms)
+        for b in range(4):
+            act(W("fh", 256 * b, 256 * b + 256), W("pa", 512 * b, 512 * b + 256), scale=0.5)
+        act(W("o1", 512, 576), ind(W("jt", 0, 256), W("l1", 32, 36)))
+        tr(W("t1", 512, 576), W("o1", 512, 576))
+        for n in range(1, 5):
+            half_step(n)
+        fi, eq, k4 = [lambda a, b, k=k: W(k, a, b) for k in ("fi", "eq", "k4")]
+        tt(eq(0, 16), fi(0, 16), fi(16, 32), A.is_equal)
+        tt(eq(16, 28), fi(16, 28), fi(4, 16), A.is_equal)
+        ts(fi(32, 64), fi(0, 32), 256.0, A.mult)
+        tt(eq(32, 44), eq(0, 12), eq(16, 28), A.add)
+        tt(W("ob", 0, 32, 2), fi(0, 16), fi(48, 64), A.add)
+        tt(eq(44, 48), eq(32, 36), eq(36, 40), A.add)
+        tt(eq(48, 52), eq(40, 44), eq(12, 16), A.add)
+        tt(W("ob", 32, 56, 2), fi(16, 28), fi(36, 48), A.add)
+        tt(eq(52, 56), eq(44, 48), eq(48, 52), A.add)
+        tt(W("ob", 56, 64, 2), fi(28, 32), fi(44, 48), A.add)
+        ts(eq(56, 60), eq(52, 56), 512.0, A.mult)
+        tt(k4(0, 4), eq(56, 60), W("pl", 0, 4), A.add)
+        for a in range(8):
+            cp(W("ob", 8 * a + 1, 8 * a + 8, 2), k4(0, 4))
+        for a in range(8):
+            dma("Y" if a % 2 else "S", "dK", W("gb", 0, 64, 1, 16 * a, 16 * a + 16), W("ob", 8 * blk(a), 8 * blk(a) + 8))
+        ts(k4(4, 8), k4(0, 4), -1.0, A.mult)
+        ts(W("fq", 0, 1024), W("fh", 0, 1024), 0.5, A.mult)
+        ts(W("fr", 0, 1024), W("fh", 0, 1024), 0.5, A.mult)
+        cp(W("gk", 0, 32), W("gb", 1, 64, 2))
+        act(W("kr", 208, 416), ind(W("id1", 0, 4096), W("gk", 16, 29)))
+        cp(W("kr", 0, 208), ind(W("id1", 0, 4096), W("gk", 0, 13)))
+        for i in range(1, 4):
+            act(W("dum", 416 * i - 416, 416 * i), W("kr", 0, 416), AF.Sign, bias=k4(4 + i, 5 + i), acc=k4(8 + i, 9 + i))
+        ts(W("cmp", 0, 416), W("kr", 0, 416), k4(0, 1), A.is_lt)
+        red(k4(8, 9), W("cmp", 0, 416), A.add)
+        cp(W("rk", 0, 1), k4(8, 9))
+        ts(W("iab", 0, 32), W("gb", 0, 64, 2), 255, A.bitwise_and)
+        ts(W("iab", 32, 64), W("gb", 0, 64, 2), 8, A.arith_shift_right)
+        ts(W("iab", 64, 96), W("gb", 1, 64, 2), 511, A.bitwise_and)
+        ts(W("rk", 1, 4), k4(9, 12), -0.5, A.mult, 207.5, A.add)
+        for a in range(8):
+            dma("Y" if a % 2 else "S", "dR", W("gr", 0, 32, 1, 16 * a, 16 * a + 16), W("rk", 0, 4))
+        cp(W("lsb", 0, 32), W("iab", 32, 64))
+        cp(W("lsa", 0, 32), W("iab", 0, 32))
+        cp(W("lsp", 0, 32), W("iab", 64, 96))
+        for c0, c1, e0, e1 in HALF:
+            act(W("br", e0, e1), ind(W("b256", 0, 256), W("lsb", c0, c1)))
+            cp(W("ar", e0, e1), ind(W("ic", 0, 256), W("lsa", c0, c1)))
+        tt(W("z2r", 0, 416), W("ar", 0, 416), W("br", 0, 416), A.add)
+        act(W("z1r", 0, 416), W("ar", 0, 416), scale=1024.0)
+        for c0, c1, e0, e1 in HALF:
+            act(W("plr", e0, e1), ind(W("id1", 0, 512), W("lsp", c0, c1)))
+        cp(W("lr", 0, 32), W("gr", 0, 32))
+        for c0, c1, e0, e1 in HALF:
+            cp(ind(W("z2s", 0, 416), W("lr", c0, c1)), W("z2r", e0, e1))
+        fold(W(lo, 0, 6), 6, W("z2s", 0, 96), 96, "fm")
+        send(relB, W("rl%d" % r, 0, 8), W(lo, 0, 8), "aL%d" % r)
+        landed("fc%d" % r, 256, "bC%d" % r)
+        landed("fs%d" % r, 256, "bS%d" % r)
+        for b in range(4):
+            mm(W("pb", 512 * b, 512 * b + 256), qe(b)[0], qe(b)[1], W("fc%d" % r, 0, 256), W("fs%d" % r, 0, 256))
+        tt(W("z1r", 0, 416), W("z1r", 0, 416), W("plr", 0, 416), A.add)
+        for c0, c1, e0, e1 in HALF:
+            cp(ind(W("z1s", 0, 416), W("lr", c0, c1)), W("z1r", e0, e1))
+        for c0, c1, e0, e1 in HALF:
+            cp(ind(W("sbw", 0, 416), W("lsp", c0, c1)), W("br", e0, e1))
+        cp(W("zi", 0, 96), W("z1s", 0, 96))
+        ts(W("pii", 0, 96), W("zi", 0, 96), 1023, A.bitwise_and)
+        ts(W("py", 0, 96), W("pii", 0, 96), 128.0, A.mult)
+        tt(W("py", 0, 96), W("py", 0, 96), W("i96", 0, 96), A.add)
+        for k in range(16):
+            z = W("ab", 320 * (k % 4), 320 * (k % 4) + 320)
+            here = k % 8 == 7
+            if here:
+                ts(z, W("z1s", 96, 416), B10(k, 1), A.add)
+            else:
+                act(z, W("z1s", 96, 416), AF.Abs, bias=B10(k, 1))
+            if k == 2:
+                for i in range(3):
+                    red(W("low", i, i + 1), W("ab", 320 * i, 320 * i + 320), A.min)
+            elif k > 2:
+                red(W("low", k, k + 1), z, A.min, here)
+        for b in range(4):
+            act(W("fp", 256 * b, 256 * b + 256), W("pb", 512 * b, 512 * b + 256), scale=0.5)
+        lt, lf, low = [lambda a, b, k=k: W(k, a, b) for k in ("lt", "lf", "low")]
+        ts(lt(0, 16), low(0, 16), 415.5, A.is_gt)
+        tt(lt(16, 32), CI(), low(0, 16), A.subtract)
+        tt(lt(32, 48), lt(0, 16), lt(16, 32), A.mult)
+        tt(lt(48, 64), lt(32, 48), low(0, 16), A.add)
+        cp(W("lsl", 0, 16), lt(48, 64))
+        cp(W("brr", 0, 256), ind(W("sbw", 0, 672), W("lsl", 0, 16)))
+        fold(lt(0, 16), 16, W("brr", 0, 256), 256, "fm2")
+        cp(W("lbl", 0, 16), lt(0, 16))
+        for b in range(4):
+            tt(W("hl", 352 * b, 352 * b + 256), ind(W("fq", 256 * b, 256 * b + 256), W("lbl", 0, 16)), W("fr", 256 * b, 256 * b + 256), A.add)
+        landed(la, 8, "bL%d" % r)
+        ts(W("ia", 8, 16), W(la, 0, 8), 8, A.arith_shift_right)
+        ts(W("ia", 0, 8), W(la, 0, 8), 255, A.bitwise_and)
+        cp(W("lbb", 0, 8), W("ia", 8, 16))
+        cp(W("laa", 0, 8), W("ia", 0, 8))
+        fp = lambda b, l: ind(W("fp", 256 * b, 256 * b + 256), W(l, 0, 6))
+        for b in range(4):
+            act(W("tb", 96 * b, 96 * b + 96), fp(b, "lbb"))
+        tt(W("zy", 0, 96), ind(W("a17", 0, 256), W("laa", 0, 6)), W("py", 0, 96), A.add)
+        for b in range(4):
+            tt(W("at", b, 384, 4), fp(b, "laa"), W("tb", 96 * b, 96 * b + 96), A.add)
+        quant(W("qa", 0, 128), W("qas", 0, 128), W("at", 0, 512))
+        for b in range(4):
+            mm(W("pa", 512 * b, 512 * b + 128), W("wq", 128 * b, 128 * b + 128), W("wqs", 128 * b, 128 * b + 128), W("qa", 0, 128), W("qas", 0, 128))
+        for k in range(16):
+            z = W("aa", 96 * (k % 4), 96 * (k % 4) + 96)
+            here = k % 4 == 3
+            if here:
+                ts(z, W("zy", 0, 96), B17(k, 1), A.add)
+            else:
+                act(z, W("zy", 0, 96), AF.Abs, bias=B17(k, 1))
+            red(W("lw", k, k + 1), z, A.min, here)
+            if k == 9:
+                for b in range(4):
+                    act(W("hl", 352 * b + 256, 352 * b + 352), W("pa", 512 * b, 512 * b + 96), scale=2.0 ** -6)
+        ts(lf(0, 16), low(0, 16), 128.0, A.mult, 60000.0, A.min)
+        cp(W("lai", 0, 16), W("lw", 0, 16))
+        tt(lf(16, 32), W("lw", 0, 16), lf(0, 16), A.is_lt)
+        ts(W("lai", 16, 32), W("lai", 0, 16), 127, A.bitwise_and)
+        tt(lf(32, 48), W("lai", 16, 32), CWM(), A.subtract)
+        tt(lf(48, 64), lf(32, 48), lf(16, 32), A.mult)
+        tt(lt(0, 16), lf(48, 64), CW(), A.add)
+        cp(W("lfl", 0, 16), lt(0, 16))
+        for b in range(4):
+            tt(W("mt", b, 1024, 4), ind(W("hl", 352 * b, 352 * b + 352), W("lfl", 0, 16)), W("fh", 256 * b, 256 * b + 256), A.add)
+    quant(W("qc3", 0, 256), W("qs3", 0, 256), W("mt", 0, 1024))
+    dma("Y", "dO", ext(T.oc[:, :]), u8(W("qc3", 0, 256)))
+    for k in range(4):
+        dma("Y", "dO", ext(T.osc[4 * k:4 * k + 4, :]), W("qs3", 0, 256, 1, 32 * k, 32 * k + 4))
+    mm(W("pa", 0, 256), W("qv", 0, 128), W("qvs", 0, 128), W("qc3", 0, 256), W("qs3", 0, 256))
+    act(W("yo", 0, 256), W("pa", 0, 256))
+    dma("S", "dO", ext(T.y[:, :]), W("yo", 0, 256))
+    next_chains()
+    for c0, c1, e0, e1 in HALF:
+        cp(W("ar", e0, e1), ind(W("z1s", 0, 416), W("lr", c0, c1)))
+    for c0, c1, e0, e1 in HALF:
+        cp(ind(W("br", 0, 416), W("lsp", c0, c1)), W("ar", e0, e1))
+    cp(W("kri", 0, 416), W("br", 0, 416))
+    ts(W("kri", 0, 416), W("kri", 0, 416), 10, A.arith_shift_right)
+    cp(W("ado", 0, 416), W("kri", 0, 416))
+    dma("Y", "dO", ext(T.ad[:, :]), W("ado", 0, 416, 1, 0, 128, 16))
+    for sname in sorted(total):
+        g.wait_ge(T.sem[sname], total[sname])

@@ -5,6 +5,7 @@ AF = ActivationFunctionType
 C, J, K, R = 256, 416, 96, 3
 F32, BF, I32, U16, CODE, U8 = "float32", "bfloat16", "int32", "uint16", "float8_e4m3fn_x4", "uint8"
 BIGID, UNIT, LOW = 2.0 ** 80, 2.0 ** 72, 9.0e29
+WAKE, SLACK, CYC, AWAY = 0.1, 0.03, 0.00083, 9.0
 SCRATCH, PLACE = {}, {}
 
 
@@ -33,10 +34,9 @@ for _t in range(R):
     _b(I32, **{"lo%d" % _t: 8, "rl%d" % _t: 8, "la%d" % _t: 8})
 _b(F32, ic=256, m16=256, enc=256, encs=256, cmax=256, fm=256, fm2=256, a1k=256, a17=256, b256=256, id1=4096,
    tab=256, bt=256, jt=256, nbv=288, d1=128, ns=288, tw=512, ti=512, o0=576, o1=576, t0=576, t1=576, kr=416, plr=416,
-   dum=1248, cmp=416, ar=416, br=416, z2r=416, z1r=416, z2s=416, z1s=416, fa=256, fb=256, ab=1280, sbw=672, brr=256, aa=384,
-   zt=416, yo=256, ado=416)
-_small(F32, "pf", wcs=96, i96=96, cst=16, pl0=32, jb=32, fl0=64, fl1=64, sm=192, fi=64, eq=64, k4=16, low=16, lt=64, py=96, zy=96,
-       lw=16, lf=64)
+   dum=1248, cmp=416, ar=416, br=416, z2r=416, z1r=416, z2s=416, z1s=416, fa=256, fb=256, ab=2560, sco=2560, sca=768, sbw=672,
+   brr=256, aa=768, zt=416, yo=256, ado=416)
+_small(F32, "pf", wcs=96, i96=96, cst=16, pl0=32, jb=32, fl0=64, fl1=64, sm=192, fi=64, eq=64, k4=16, lt=64, py=96, zy=96, lf=64)
 _b(I32, pi=16, s2=8, s8=8, nsi=8, kri=416)
 _small(I32, "qi", nbi=16, pin=32, cz=32, zc=32, ids=32, sw4=16, pl=4, ob=64, gb=64, iab=96, rk=4, gr=32, zi=96, pii=96, ia=16, lai=32)
 _b(U16, lu=8, lb=8)
@@ -87,7 +87,7 @@ def rank_program(g, core, T, topo):
         return
     V, S, TE = g.vector, g.scalar, g.tensor
     eng = {"V": V, "S": S, "T": TE, "G": g, "Y": g.sync}
-    total, known, recs = {}, {}, {}
+    calls, known, recs = [], {}, {}
 
     def W(name, a, b, step=1, p0=0, p1=128, ps=1):
         if name in PLACE:
@@ -99,88 +99,146 @@ def rank_program(g, core, T, topo):
         else:
             ap = t[p0:p1, a:b] if ps == 1 else t[p0:p1:ps, a:b]
         if name in ("pa", "pb"):
-            a, b = a // 512 * 512, (b + 511) // 512 * 512
-        return {"ap": ap, "reg": (name, p0, p1, a, b, step, a % step), "aux": []}
+            return {"ap": ap, "reg": (name, p0, p1, a // 512 * 512, (b + 511) // 512 * 512, 1, 0), "aux": [], "n": b - a}
+        return {"ap": ap, "reg": (name, p0, p1, a, b, step, a % step), "aux": [], "n": (b - a + step - 1) // step}
 
     def ind(win, lst):
-        return {"ap": win["ap"].indirect(lst["ap"]), "reg": win["reg"], "aux": [lst["reg"]]}
+        return {"ap": win["ap"].indirect(lst["ap"]), "reg": win["reg"], "aux": [lst["reg"]], "n": 0}
 
     def u8(v):
-        return {"ap": v["ap"].bitcast(dt.uint8), "reg": v["reg"], "aux": []}
+        return dict(v, ap=v["ap"].bitcast(dt.uint8))
 
     def u32(v):
-        return {"ap": v["ap"].bitcast(dt.uint32), "reg": v["reg"], "aux": []}
+        return dict(v, ap=v["ap"].bitcast(dt.uint32))
 
     def ext(x):
-        return {"ap": x, "reg": None, "aux": []}
+        return {"ap": x, "reg": None, "aux": [], "n": 0}
 
     def meet(r, o):
         if r[5] > 1 and r[5] == o[5] and r[6] != o[6]:
             return False
         return r[1] < o[2] and o[1] < r[2] and r[3] < o[4] and o[3] < r[4]
 
-    def op(q, fn, outs, ins, sem=None, val=None):
+    def op(q, fn, outs, ins, cost, sem=None, val=None, lat=0.0, after=()):
         rd = [r for v in ins for r in [v["reg"]] + v["aux"] if r] + [r for v in outs for r in v["aux"]]
         wr = [v["reg"] for v in outs if v["reg"]] + [r for r in rd if r[0] in ("pa", "pb")]
         me = sem if sem else "s" + q
-        need = {}
+        deps, n = set(after), len(calls)
         for kind, regs in (("r", rd), ("w", wr)):
             for r in regs:
-                for o, ok, os_, ov in recs.get(r[0], []):
+                for o, ok, k in recs.get(r[0], []):
                     if not meet(r, o) or (kind == "r" and ok == "r"):
                         continue
-                    if kind == "w" and ok == "w" and os_ == me and me in DMAS:
+                    if kind == "w" and ok == "w" and calls[k]["me"] == me and me in DMAS:
                         continue
-                    need[os_] = max(need.get(os_, 0), total[os_] if os_ in DMAS else ov)
-        kn = known.setdefault(q, {})
-        for s in sorted(need):
-            if kn.get(s, 0) < need[s]:
-                eng[q].wait_ge(T.sem[s], need[s])
-                kn[s] = need[s]
-        c = fn()
+                    deps.add(k)
+        whole = {}
+        for s in set(calls[k]["me"] for k in deps if calls[k]["me"] in DMAS):
+            mine = [k for k in range(n) if calls[k]["me"] == s]
+            deps.update(mine)
+            whole[s] = 16 * len(mine)
         amount = val if val else 16 if me in DMAS else 1
-        if val is None:
-            c.then_inc(T.sem[me], amount)
-        total[me] = total.get(me, 0) + amount
+        calls.append({"q": q, "fn": fn, "me": me, "n": amount, "inc": val is None, "deps": deps, "whole": whole, "cost": cost, "lat": lat})
         for kind, regs in (("r", rd), ("w", wr)):
             for r in regs:
                 keep = []
                 for rec in recs.get(r[0], []):
                     o = rec[0]
                     inside = r[1] <= o[1] and o[2] <= r[2] and r[3] <= o[3] and o[4] <= r[4] and (r[5] == 1 or r[5:] == o[5:])
-                    if not (inside and (kind == "w" or (rec[1] == "r" and rec[2] == me))):
+                    if not (inside and kind == "w"):
                         keep.append(rec)
-                recs[r[0]] = keep + [(r, kind, me, total[me])]
+                recs[r[0]] = keep + [(r, kind, n)]
+        return n
 
-    def landed(name, n, sem):
-        recs.setdefault(name, []).append(((name, 0, 128, 0, n, 1, 0), "w", sem, 8))
+    def landed(name, n, sem, sent):
+        op("X", None, [{"reg": (name, 0, 128, 0, n, 1, 0), "aux": []}], [], 0.0, sem=sem, val=8, lat=AWAY, after=(sent,))
+
+    def issue():
+        n = len(calls)
+        succ, left, ready, way, at = [[] for _ in calls], [len(c["deps"]) for c in calls], [0.0] * n, [0.0] * n, [0] * n
+        for k, c in enumerate(calls):
+            for d in c["deps"]:
+                succ[d].append(k)
+        for k in range(n - 1, -1, -1):
+            way[k] = calls[k]["cost"] + calls[k]["lat"] + max([way[x] + WAKE for x in succ[k]] + [0.0])
+        can, free, count = {}, {}, {}
+        for k in range(n):
+            if not left[k]:
+                can.setdefault(calls[k]["q"], []).append(k)
+        for _ in range(n):
+            best = None
+            for q in sorted(can):
+                if not can[q]:
+                    continue
+                f = free.get(q, 0.0)
+                m = min(max(f, ready[k]) for k in can[q])
+                k = max((k for k in can[q] if max(f, ready[k]) <= m + SLACK), key=lambda k: (way[k], -k))
+                t = max(f, ready[k])
+                if best is None or t < best[0]:
+                    best = (t, k)
+            t, k = best
+            c = calls[k]
+            q, me = c["q"], c["me"]
+            can[q].remove(k)
+            end = t + c["cost"]
+            if q != "X":
+                free[q] = end
+                kn = known.setdefault(q, {})
+                need = dict(c["whole"])
+                for d in c["deps"]:
+                    s = calls[d]["me"]
+                    if s not in DMAS:
+                        need[s] = max(need.get(s, 0), at[d])
+                for s in sorted(need):
+                    if kn.get(s, 0) < need[s]:
+                        eng[q].wait_ge(T.sem[s], need[s])
+                        kn[s] = need[s]
+                x = c["fn"]()
+                if c["inc"]:
+                    x.then_inc(T.sem[me], c["n"])
+            count[me] = count.get(me, 0) + c["n"]
+            at[k] = count[me]
+            for x in succ[k]:
+                ready[x] = max(ready[x], end + c["lat"] + WAKE)
+                left[x] -= 1
+                if not left[x]:
+                    can.setdefault(calls[x]["q"], []).append(x)
+        for s in sorted(count):
+            g.wait_ge(T.sem[s], count[s])
+
+    def wide(v, full=1.0):
+        return max(64, full * v["n"]) * CYC
 
     def tt(out, a, b, o):
-        op("V", lambda: V.tensor_tensor(out["ap"], a["ap"], b["ap"], o), [out], [a, b])
+        cost = 0.05 + wide(b, 1.5) if a["aux"] else wide(b, 1 if a["reg"][0] in ("pa", "pb") else 2)
+        op("V", lambda: V.tensor_tensor(out["ap"], a["ap"], b["ap"], o), [out], [a, b], cost)
 
     def ts(out, a, s1, o1, s2=None, o2=None):
         ins = [a] + [s for s in (s1, s2) if isinstance(s, dict)]
         x1, x2 = [s["ap"] if isinstance(s, dict) else s for s in (s1, s2)]
         if o2 is None:
-            op("V", lambda: V.tensor_scalar(out["ap"], a["ap"], x1, None, o1), [out], ins)
+            op("V", lambda: V.tensor_scalar(out["ap"], a["ap"], x1, None, o1), [out], ins, wide(a))
         else:
-            op("V", lambda: V.tensor_scalar(out["ap"], a["ap"], x1, x2, o1, o2), [out], ins)
+            op("V", lambda: V.tensor_scalar(out["ap"], a["ap"], x1, x2, o1, o2), [out], ins, wide(a))
 
     def cp(out, a):
-        op("V", lambda: V.tensor_copy(out["ap"], a["ap"]), [out], [a])
+        cost = 0.05 + wide(out, 1.5) if a["aux"] else 0.05 + wide(a, 3) if out["aux"] else wide(a)
+        op("V", lambda: V.tensor_copy(out["ap"], a["ap"]), [out], [a], cost)
 
     def fill(out, c):
-        op("V", lambda: V.memset(out["ap"], c), [out], [])
+        op("V", lambda: V.memset(out["ap"], c), [out], [], wide(out))
 
-    def red(out, a, o, size=False):
-        kw = {"apply_absolute_value": True} if size else {}
-        op("V", lambda: V.tensor_reduce(out["ap"], a["ap"], AxisListType.X, o, **kw), [out], [a])
+    def red(out, a, o):
+        op("V", lambda: V.tensor_reduce(out["ap"], a["ap"], AxisListType.X, o), [out], [a], wide(a))
+
+    def low2(out, a, b):
+        op("V", lambda: V.tensor_tensor_scan(out["ap"], a["ap"], b["ap"], 1e29, A.min, A.min), [out], [a, b], wide(a))
 
     def tr(out, a):
-        op("V", lambda: V.transpose(out["ap"], a["ap"]), [out], [a])
+        op("V", lambda: V.transpose(out["ap"], a["ap"]), [out], [a], wide(a))
 
     def quant(q, s, x):
-        op("V", lambda: V.quantize_mx(q["ap"], s["ap"], x["ap"]), [q, s], [x])
+        op("V", lambda: V.quantize_mx(q["ap"], s["ap"], x["ap"]), [q, s], [x], 0.012 + wide(x, 0.265))
 
     def act(out, a, f=AF.Copy, scale=None, bias=None, acc=None):
         kw, ins, outs = {}, [a], [out]
@@ -192,20 +250,20 @@ def rank_program(g, core, T, topo):
         if acc is not None:
             kw["accum_out"] = acc["ap"]
             outs.append(acc)
-        op("S", lambda: S.activation(out["ap"], a["ap"], f, **kw), outs, ins)
+        op("S", lambda: S.activation(out["ap"], a["ap"], f, **kw), outs, ins, 0.065 + wide(out, 1.5 if a["aux"] else 1.0))
 
     def mm(out, l, ls, r, rs):
-        op("T", lambda: TE.matmul_mx(out["ap"], l["ap"], ls["ap"], r["ap"], rs["ap"], True, True), [out], [l, ls, r, rs])
+        op("T", lambda: TE.matmul_mx(out["ap"], l["ap"], ls["ap"], r["ap"], rs["ap"], True, True), [out], [l, ls, r, rs], 0.02 + wide(r))
 
     def dma(q, sem, out, in_):
-        op(q, lambda: eng[q].dma_start(out["ap"], in_["ap"]), [out], [in_], sem=sem)
+        op(q, lambda: eng[q].dma_start(out["ap"], in_["ap"]), [out], [in_], 0.07, sem=sem, lat=2.0)
 
     def iota(out, pat, cm):
         kw = {} if out["reg"][0] in ("pi", "s2", "s8") else {"allow_small_or_imprecise_dtypes": True}
-        op("G", lambda: g.iota(out["ap"], pat, 0, cm, **kw), [out], [])
+        op("G", lambda: g.iota(out["ap"], pat, 0, cm, **kw), [out], [], 0.13 + wide(out, 2))
 
     def send(dst, out, src, sem):
-        op("G", lambda: put(g, T, topo, core, dst, out["ap"], src["ap"], sem), [], [src], sem="snt", val=8)
+        return op("G", lambda: put(g, T, topo, core, dst, out["ap"], src["ap"], sem), [], [src], 0.1, sem="snt", val=8)
 
     def fold(out, n_out, src, n, mask):
         tt(W("fa", 0, n), src, W(mask, 0, n), A.mult)
@@ -242,7 +300,7 @@ def rank_program(g, core, T, topo):
     fill(W("ones", 0, 512), 1.0)
     for b in range(4):
         o, i = W("eb", 512 * b, 512 * b + 512), W("ones", 0, 512)
-        op("G", lambda: g.affine_select(o["ap"], i["ap"], [[-1, 512]], A.is_equal, 0.0, b, 4), [o], [i])
+        op("G", lambda o=o, i=i, b=b: g.affine_select(o["ap"], i["ap"], [[-1, 512]], A.is_equal, 0.0, b, 4), [o], [i], 1.0)
     iota(W("m16", 0, 256), [[0, 16], [1, 16]], 0)
     iota(W("wcs", 0, 16), [[16, 16]], 0)
     iota(W("i96", 0, 96), [[1, 96]], 0)
@@ -295,22 +353,20 @@ def rank_program(g, core, T, topo):
     for t in range(R):
         fill(W("lo%d" % t, 0, 8), 0)
     CW, CI, CWM, B10, B17 = [lambda k=0, n=16, o=o: W("wcs", o + k, o + k + n) for o in (0, 16, 32, 48, 64)]
-
-    def later_constants():
-        quant(W("qe", 0, 512), W("qes", 0, 512), W("eb", 0, 2048))
-        ts(W("fm", 0, 256), W("m16", 0, 256), lane, A.is_equal)
-        ts(W("a1k", 0, 256), W("ic", 0, 256), 1024.0, A.mult)
-        ts(W("fm2", 0, 256), W("fm", 0, 256), 2.0 ** -8, A.mult)
-        ts(W("b256", 0, 256), W("ic", 0, 256), 256.0, A.mult)
-        ts(CW(), CW(), lane, A.add)
-        ts(W("a17", 0, 256), W("ic", 0, 256), 2.0 ** 17, A.mult)
-        cp(W("sbw", 416, 672), W("b256", 0, 256))
-        ts(CI(), CW(), 416.0, A.add)
-        ts(CWM(), CW(), 256.0, A.subtract)
-        ts(B10(), CW(), -1024.0, A.mult)
-        ts(B17(), CW(), -2.0 ** 17, A.mult, 2.0 ** 24, A.add)
-        ts(W("i96", 0, 96), W("i96", 0, 96), 2.0 ** 24, A.subtract)
-        quant(W("qv", 0, 128), W("qvs", 0, 128), W("vt", 0, 512))
+    quant(W("qe", 0, 512), W("qes", 0, 512), W("eb", 0, 2048))
+    ts(W("fm", 0, 256), W("m16", 0, 256), lane, A.is_equal)
+    ts(W("a1k", 0, 256), W("ic", 0, 256), 1024.0, A.mult)
+    ts(W("fm2", 0, 256), W("fm", 0, 256), 2.0 ** -8, A.mult)
+    ts(W("b256", 0, 256), W("ic", 0, 256), 256.0, A.mult)
+    ts(CW(), CW(), lane, A.add)
+    ts(W("a17", 0, 256), W("ic", 0, 256), 2.0 ** 17, A.mult)
+    cp(W("sbw", 416, 672), W("b256", 0, 256))
+    ts(CI(), CW(), 416.0, A.add)
+    ts(CWM(), CW(), 256.0, A.subtract)
+    ts(B10(), CW(), -1024.0, A.mult)
+    ts(B17(), CW(), -2.0 ** 17, A.mult, 2.0 ** 24, A.add)
+    ts(W("i96", 0, 96), W("i96", 0, 96), 2.0 ** 24, A.subtract)
+    quant(W("qv", 0, 128), W("qvs", 0, 128), W("vt", 0, 512))
 
     def code(out, x):
         ts(out, x, 1 / UNIT, A.mult, 256.0, A.subtract)
@@ -377,8 +433,8 @@ def rank_program(g, core, T, topo):
         q, s, lo, la = "qc%d" % r, "qs%d" % r, "lo%d" % r, "la%d" % r
         if r:
             quant(W(q, 0, 256), W(s, 0, 256), W("mt", 0, 1024))
-        send(relA, u8(W("rc%d" % r, 0, 256)), u8(W(q, 0, 256)), "aC%d" % r)
-        send(relB, W("rs%d" % r, 0, 256), W(s, 0, 256), "aS%d" % r)
+        s1 = send(relA, u8(W("rc%d" % r, 0, 256)), u8(W(q, 0, 256)), "aC%d" % r)
+        s2 = send(relB, W("rs%d" % r, 0, 256), W(s, 0, 256), "aS%d" % r)
         if r == 0:
             iota(W("id1", 0, 4096), [[1, 4096]], 0)
         mq, ms = W(q, 0, 256), W(s, 0, 256)
@@ -414,7 +470,7 @@ def rank_program(g, core, T, topo):
         tt(W("jb", 0, 32, 2), ti(64, 80), W("nbv", 256, 272), A.add)
         tt(W("jb", 1, 32, 2), ti(80, 96), W("nbv", 272, 288), A.add)
         for h in range(8):
-            dma("Y", "dJ", W("jt", 32 * h, 32 * h + 32, 1, 0, 128, 8), W("jb", 0, 32, 1, 16 * h, 16 * h + 16))
+            dma("Y" if h % 2 else "S", "dJ", W("jt", 32 * h, 32 * h + 32, 1, 0, 128, 8), W("jb", 0, 32, 1, 16 * h, 16 * h + 16))
         ts(W("ids", 0, 32), W("zc", 0, 32), 10, A.arith_shift_right)
         cp(W("l1", 0, 32), W("ids", 0, 32))
         act(W("o1", 256, 512), ind(W("tab", 0, 256), W("l1", 16, 32)))
@@ -427,8 +483,6 @@ def rank_program(g, core, T, topo):
         ts(W("pl", 0, 4), W("zc", 0, 4), 1023, A.bitwise_and)
         tr(W("t1", 0, 256), W("o1", 0, 256))
         tr(W("t1", 256, 512), W("o1", 256, 512))
-        if r == 0:
-            later_constants()
         qe = lambda b: (W("qe", 128 * b, 128 * b + 128), W("qes", 128 * b, 128 * b + 128))
         for b in range(4):
             mm(W("pa", 512 * b, 512 * b + 256), qe(b)[0], qe(b)[1], mq, ms)
@@ -486,9 +540,9 @@ def rank_program(g, core, T, topo):
         for c0, c1, e0, e1 in HALF:
             cp(ind(W("z2s", 0, 416), W("lr", c0, c1)), W("z2r", e0, e1))
         fold(W(lo, 0, 6), 6, W("z2s", 0, 96), 96, "fm")
-        send(relB, W("rl%d" % r, 0, 8), W(lo, 0, 8), "aL%d" % r)
-        landed("fc%d" % r, 256, "bC%d" % r)
-        landed("fs%d" % r, 256, "bS%d" % r)
+        s3 = send(relB, W("rl%d" % r, 0, 8), W(lo, 0, 8), "aL%d" % r)
+        landed("fc%d" % r, 256, "bC%d" % r, s1)
+        landed("fs%d" % r, 256, "bS%d" % r, s2)
         for b in range(4):
             mm(W("pb", 512 * b, 512 * b + 256), qe(b)[0], qe(b)[1], W("fc%d" % r, 0, 256), W("fs%d" % r, 0, 256))
         tt(W("z1r", 0, 416), W("z1r", 0, 416), W("plr", 0, 416), A.add)
@@ -501,31 +555,24 @@ def rank_program(g, core, T, topo):
         ts(W("py", 0, 96), W("pii", 0, 96), 128.0, A.mult)
         tt(W("py", 0, 96), W("py", 0, 96), W("i96", 0, 96), A.add)
         for k in range(16):
-            z = W("ab", 320 * (k % 4), 320 * (k % 4) + 320)
-            here = k % 8 == 7
-            if here:
-                ts(z, W("z1s", 96, 416), B10(k, 1), A.add)
-            else:
-                act(z, W("z1s", 96, 416), AF.Abs, bias=B10(k, 1))
-            if k == 2:
-                for i in range(3):
-                    red(W("low", i, i + 1), W("ab", 320 * i, 320 * i + 320), A.min)
-            elif k > 2:
-                red(W("low", k, k + 1), z, A.min, here)
+            o = 320 * (k % 8)
+            act(W("ab", o, o + 320), W("z1s", 96, 416), AF.Abs, bias=B10(k, 1))
+            low2(W("sco", 160 * k, 160 * k + 160), W("ab", o, o + 160), W("ab", o + 160, o + 320))
         for b in range(4):
             act(W("fp", 256 * b, 256 * b + 256), W("pb", 512 * b, 512 * b + 256), scale=0.5)
-        lt, lf, low = [lambda a, b, k=k: W(k, a, b) for k in ("lt", "lf", "low")]
-        ts(lt(0, 16), low(0, 16), 415.5, A.is_gt)
-        tt(lt(16, 32), CI(), low(0, 16), A.subtract)
+        lt, lf = [lambda a, b, k=k: W(k, a, b) for k in ("lt", "lf")]
+        low, lowa = W("sco", 159, 2560, 160), W("sca", 47, 768, 48)
+        ts(lt(0, 16), low, 415.5, A.is_gt)
+        tt(lt(16, 32), CI(), low, A.subtract)
         tt(lt(32, 48), lt(0, 16), lt(16, 32), A.mult)
-        tt(lt(48, 64), lt(32, 48), low(0, 16), A.add)
+        tt(lt(48, 64), lt(32, 48), low, A.add)
         cp(W("lsl", 0, 16), lt(48, 64))
         cp(W("brr", 0, 256), ind(W("sbw", 0, 672), W("lsl", 0, 16)))
         fold(lt(0, 16), 16, W("brr", 0, 256), 256, "fm2")
         cp(W("lbl", 0, 16), lt(0, 16))
         for b in range(4):
             tt(W("hl", 352 * b, 352 * b + 256), ind(W("fq", 256 * b, 256 * b + 256), W("lbl", 0, 16)), W("fr", 256 * b, 256 * b + 256), A.add)
-        landed(la, 8, "bL%d" % r)
+        landed(la, 8, "bL%d" % r, s3)
         ts(W("ia", 8, 16), W(la, 0, 8), 8, A.arith_shift_right)
         ts(W("ia", 0, 8), W(la, 0, 8), 255, A.bitwise_and)
         cp(W("lbb", 0, 8), W("ia", 8, 16))
@@ -540,19 +587,14 @@ def rank_program(g, core, T, topo):
         for b in range(4):
             mm(W("pa", 512 * b, 512 * b + 128), W("wq", 128 * b, 128 * b + 128), W("wqs", 128 * b, 128 * b + 128), W("qa", 0, 128), W("qas", 0, 128))
         for k in range(16):
-            z = W("aa", 96 * (k % 4), 96 * (k % 4) + 96)
-            here = k % 4 == 3
-            if here:
-                ts(z, W("zy", 0, 96), B17(k, 1), A.add)
-            else:
-                act(z, W("zy", 0, 96), AF.Abs, bias=B17(k, 1))
-            red(W("lw", k, k + 1), z, A.min, here)
-            if k == 9:
-                for b in range(4):
-                    act(W("hl", 352 * b + 256, 352 * b + 352), W("pa", 512 * b, 512 * b + 96), scale=2.0 ** -6)
-        ts(lf(0, 16), low(0, 16), 128.0, A.mult, 60000.0, A.min)
-        cp(W("lai", 0, 16), W("lw", 0, 16))
-        tt(lf(16, 32), W("lw", 0, 16), lf(0, 16), A.is_lt)
+            o = 96 * (k % 8)
+            act(W("aa", o, o + 96), W("zy", 0, 96), AF.Abs, bias=B17(k, 1))
+            low2(W("sca", 48 * k, 48 * k + 48), W("aa", o, o + 48), W("aa", o + 48, o + 96))
+        for b in range(4):
+            act(W("hl", 352 * b + 256, 352 * b + 352), W("pa", 512 * b, 512 * b + 96), scale=2.0 ** -6)
+        ts(lf(0, 16), low, 128.0, A.mult, 60000.0, A.min)
+        cp(W("lai", 0, 16), lowa)
+        tt(lf(16, 32), lowa, lf(0, 16), A.is_lt)
         ts(W("lai", 16, 32), W("lai", 0, 16), 127, A.bitwise_and)
         tt(lf(32, 48), W("lai", 16, 32), CWM(), A.subtract)
         tt(lf(48, 64), lf(32, 48), lf(16, 32), A.mult)
@@ -576,5 +618,4 @@ def rank_program(g, core, T, topo):
     ts(W("kri", 0, 416), W("kri", 0, 416), 10, A.arith_shift_right)
     cp(W("ado", 0, 416), W("kri", 0, 416))
     dma("Y", "dO", ext(T.ad[:, :]), W("ado", 0, 416, 1, 0, 128, 16))
-    for sname in sorted(total):
-        g.wait_ge(T.sem[sname], total[sname])
+    issue()

from concourse.mybir import dt, AluOpType, AxisListType, ActivationFunctionType

A = AluOpType
AF = ActivationFunctionType
C, J, K, R = 256, 416, 96, 3
F32, BF, I32, U16, CODE, U8 = "float32", "bfloat16", "int32", "uint16", "float8_e4m3fn_x4", "uint8"
BIGID, UNIT, LOW = 2.0 ** 80, 2.0 ** 72, 9.0e29
WAKE, SLACK, CYC, AWAY = 0.1, 0.03, 0.00083, 9.0
SCRATCH, PLACE = {}, {}


def _b(dtype, **sizes):
    for k, n in sizes.items():
        SCRATCH[k] = ("sbuf", [128, n], dtype)


def _small(dtype, buf, **sizes):
    at = 0
    for k, n in sizes.items():
        PLACE[k] = (buf, at)
        at += (n + 31) // 32 * 32
    SCRATCH[buf] = ("sbuf", [128, at], dtype)


_b(BF, xt=1024, mt=1024, ut=512, vt=512, ones=512, eb=2048, fh=1024, fq=1024, fr=1024, fp=1024, hl=1408, at=512, tb=384)
_b(CODE, qu=128, qv=128, uq=128, bq=128, qe=512, wq=512, qa=128)
_b(U8, qus=128, qvs=128, uqs=128, bqs=128, qes=512, wqs=512, qas=128)
for _t in range(R + 1):
    _b(CODE, **{"qc%d" % _t: 256})
    _b(U8, **{"qs%d" % _t: 256})
for _t in range(R):
    _b(CODE, **{"rc%d" % _t: 256, "fc%d" % _t: 256})
    _b(U8, **{"rs%d" % _t: 256, "fs%d" % _t: 256})
    _b(I32, **{"lo%d" % _t: 8, "rl%d" % _t: 8, "la%d" % _t: 8})
_b(F32, ic=256, m16=256, enc=256, encs=256, cmax=256, fm=256, fm2=256, a1k=256, a17=256, b256=256, id1=4096,
   tab=256, bt=256, jt=256, nbv=288, d1=128, ns=288, tw=512, ti=512, o0=576, o1=576, t0=576, t1=576, kr=416, plr=416,
   dum=1248, cmp=416, ar=416, br=416, z2r=416, z1r=416, z2s=416, z1s=416, fa=256, fb=256, ab=2560, sco=2560, sca=768, sbw=672,
   brr=256, aa=768, zt=416, yo=256, ado=416)
_small(F32, "pf", wcs=96, i96=96, cst=16, pl0=32, jb=32, fl0=64, fl1=64, sm=192, fi=64, eq=64, k4=16, lt=64, py=96, zy=96, lf=64)
_b(I32, pi=16, s2=8, s8=8, nsi=8, kri=416)
_small(I32, "qi", nbi=16, pin=32, cz=32, zc=32, ids=32, sw4=16, pl=4, ob=64, gb=64, iab=96, rk=4, gr=32, zi=96, pii=96, ia=16, lai=32)
_b(U16, lu=8, lb=8)
_small(U16, "pu", nbl=18, l0=40, l1=40, gk=32, lsa=32, lsb=32, lsp=32, lr=32, laa=8, lbb=8, lsl=16, lbl=16, lfl=16)
SCRATCH["pa"] = ("psum", [128, 2048], F32)
SCRATCH["pb"] = ("psum", [128, 2048], F32)
DMAS = ["dX", "dU", "dW", "dV", "dN", "dP", "dJ", "dK", "dR", "dZ", "dO"]
SEMAPHORES = ["sV", "sS", "sT", "sG", "snt"] + DMAS + [k + str(t) for t in range(R) for k in ("aC", "aS", "aL", "bC", "bS", "bL")]
HALF = ((0, 13, 0, 208), (16, 29, 208, 416))


def relays(topo, cores, r):
    src, dst = cores[r], cores[(r + 1) % len(cores)]
    ok = [c for c in topo.cores_of(src) if c not in cores and topo.may_write(c, dst)]
    ok.sort(key=lambda c: (topo.die(c) != topo.die(src), c))
    return ok[0], ok[1]


def put(g, T, topo, core, dst, out, in_, sem):
    rid, pid = topo.addr(dst, core)
    g.remote_dma(out, in_, T.sem[sem], T.sem.snt, pid, rid, sum(1 << k for k in topo.engines(core, dst)[:8]))


def relay_program(g, core, T, topo):
    n, sent = len(T.cores), 0
    for r in range(n):
        a, b = relays(topo, T.cores, r)
        dst = T.cores[(r + 1) % n]
        for t in range(R):
            if core == a:
                g.wait_ge(T.sem["aC%d" % t], 8)
                put(g, T, topo, core, dst, T["fc%d" % t][:, 0:C].bitcast(dt.uint8), T["rc%d" % t][:, 0:C].bitcast(dt.uint8), "bC%d" % t)
                sent += 8
            if core == b:
                g.wait_ge(T.sem["aS%d" % t], 8)
                put(g, T, topo, core, dst, T["fs%d" % t][:, 0:C], T["rs%d" % t][:, 0:C], "bS%d" % t)
                g.wait_ge(T.sem["aL%d" % t], 8)
                put(g, T, topo, core, dst, T["la%d" % t][:, 0:8], T["rl%d" % t][:, 0:8], "bL%d" % t)
                sent += 16
    if sent:
        g.wait_ge(T.sem.snt, sent)


def rank_program(g, core, T, topo):
    rank = T.rank_of(core)
    if rank is None:
        relay_program(g, core, T, topo)
        return
    V, S, TE = g.vector, g.scalar, g.tensor
    eng = {"V": V, "S": S, "T": TE, "G": g, "Y": g.sync}
    calls, known, recs = [], {}, {}

    def W(name, a, b, step=1, p0=0, p1=128, ps=1):
        if name in PLACE:
            name, o = PLACE[name]
            a, b = a + o, b + o
        t = T[name]
        if (p0, p1, ps) == (0, 128, 1):
            ap = t[:, a:b] if step == 1 else t[:, a:b:step]
        else:
            ap = t[p0:p1, a:b] if ps == 1 else t[p0:p1:ps, a:b]
        if name in ("pa", "pb"):
            return {"ap": ap, "reg": (name, p0, p1, a // 512 * 512, (b + 511) // 512 * 512, 1, 0), "aux": [], "n": b - a}
        return {"ap": ap, "reg": (name, p0, p1, a, b, step, a % step), "aux": [], "n": (b - a + step - 1) // step}

    def ind(win, lst):
        return {"ap": win["ap"].indirect(lst["ap"]), "reg": win["reg"], "aux": [lst["reg"]], "n": 0}

    def u8(v):
        return dict(v, ap=v["ap"].bitcast(dt.uint8))

    def u32(v):
        return dict(v, ap=v["ap"].bitcast(dt.uint32))

    def ext(x):
        return {"ap": x, "reg": None, "aux": [], "n": 0}

    def meet(r, o):
        if r[5] > 1 and r[5] == o[5] and r[6] != o[6]:
            return False
        return r[1] < o[2] and o[1] < r[2] and r[3] < o[4] and o[3] < r[4]

    def op(q, fn, outs, ins, cost, sem=None, val=None, lat=0.0, after=()):
        rd = [r for v in ins for r in [v["reg"]] + v["aux"] if r] + [r for v in outs for r in v["aux"]]
        wr = [v["reg"] for v in outs if v["reg"]] + [r for r in rd if r[0] in ("pa", "pb")]
        me = sem if sem else "s" + q
        deps, n = set(after), len(calls)
        for kind, regs in (("r", rd), ("w", wr)):
            for r in regs:
                for o, ok, k in recs.get(r[0], []):
                    if not meet(r, o) or (kind == "r" and ok == "r"):
                        continue
                    if kind == "w" and ok == "w" and calls[k]["me"] == me and me in DMAS:
                        continue
                    deps.add(k)
        whole = {}
        for s in set(calls[k]["me"] for k in deps if calls[k]["me"] in DMAS):
            mine = [k for k in range(n) if calls[k]["me"] == s]
            deps.update(mine)
            whole[s] = 16 * len(mine)
        amount = val if val else 16 if me in DMAS else 1
        calls.append({"q": q, "fn": fn, "me": me, "n": amount, "inc": val is None, "deps": deps, "whole": whole, "cost": cost, "lat": lat})
        for kind, regs in (("r", rd), ("w", wr)):
            for r in regs:
                keep = []
                for rec in recs.get(r[0], []):
                    o = rec[0]
                    inside = r[1] <= o[1] and o[2] <= r[2] and r[3] <= o[3] and o[4] <= r[4] and (r[5] == 1 or r[5:] == o[5:])
                    if not (inside and kind == "w"):
                        keep.append(rec)
                recs[r[0]] = keep + [(r, kind, n)]
        return n

    def landed(name, n, sem, sent):
        op("X", None, [{"reg": (name, 0, 128, 0, n, 1, 0), "aux": []}], [], 0.0, sem=sem, val=8, lat=AWAY, after=(sent,))

    def issue():
        n = len(calls)
        succ, left, ready, way, at = [[] for _ in calls], [len(c["deps"]) for c in calls], [0.0] * n, [0.0] * n, [0] * n
        for k, c in enumerate(calls):
            for d in c["deps"]:
                succ[d].append(k)
        for k in range(n - 1, -1, -1):
            way[k] = calls[k]["cost"] + calls[k]["lat"] + max([way[x] + WAKE for x in succ[k]] + [0.0])
        can, free, count = {}, {}, {}
        for k in range(n):
            if not left[k]:
                can.setdefault(calls[k]["q"], []).append(k)
        for _ in range(n):
            best = None
            for q in sorted(can):
                if not can[q]:
                    continue
                f = free.get(q, 0.0)
                m = min(max(f, ready[k]) for k in can[q])
                k = max((k for k in can[q] if max(f, ready[k]) <= m + SLACK), key=lambda k: (way[k], -k))
                t = max(f, ready[k])
                if best is None or t < best[0]:
                    best = (t, k)
            t, k = best
            c = calls[k]
            q, me = c["q"], c["me"]
            can[q].remove(k)
            end = t + c["cost"]
            if q != "X":
                free[q] = end
                kn = known.setdefault(q, {})
                need = dict(c["whole"])
                for d in c["deps"]:
                    s = calls[d]["me"]
                    if s not in DMAS:
                        need[s] = max(need.get(s, 0), at[d])
                for s in sorted(need):
                    if kn.get(s, 0) < need[s]:
                        eng[q].wait_ge(T.sem[s], need[s])
                        kn[s] = need[s]
                x = c["fn"]()
                if c["inc"]:
                    x.then_inc(T.sem[me], c["n"])
            count[me] = count.get(me, 0) + c["n"]
            at[k] = count[me]
            for x in succ[k]:
                ready[x] = max(ready[x], end + c["lat"] + WAKE)
                left[x] -= 1
                if not left[x]:
                    can.setdefault(calls[x]["q"], []).append(x)
        for s in sorted(count):
            g.wait_ge(T.sem[s], count[s])

    def wide(v, full=1.0):
        return max(64, full * v["n"]) * CYC

    def tt(out, a, b, o):
        cost = 0.05 + wide(b, 1.5) if a["aux"] else wide(b, 1 if a["reg"][0] in ("pa", "pb") else 2)
        op("V", lambda: V.tensor_tensor(out["ap"], a["ap"], b["ap"], o), [out], [a, b], cost)

    def ts(out, a, s1, o1, s2=None, o2=None):
        ins = [a] + [s for s in (s1, s2) if isinstance(s, dict)]
        x1, x2 = [s["ap"] if isinstance(s, dict) else s for s in (s1, s2)]
        if o2 is None:
            op("V", lambda: V.tensor_scalar(out["ap"], a["ap"], x1, None, o1), [out], ins, wide(a))
        else:
            op("V", lambda: V.tensor_scalar(out["ap"], a["ap"], x1, x2, o1, o2), [out], ins, wide(a))

    def cp(out, a):
        cost = 0.05 + wide(out, 1.5) if a["aux"] else 0.05 + wide(a, 3) if out["aux"] else wide(a)
        op("V", lambda: V.tensor_copy(out["ap"], a["ap"]), [out], [a], cost)

    def fill(out, c):
        op("V", lambda: V.memset(out["ap"], c), [out], [], wide(out))

    def red(out, a, o):
        op("V", lambda: V.tensor_reduce(out["ap"], a["ap"], AxisListType.X, o), [out], [a], wide(a))

    def low2(out, a, b):
        op("V", lambda: V.tensor_tensor_scan(out["ap"], a["ap"], b["ap"], 1e29, A.min, A.min), [out], [a, b], wide(a))

    def tr(out, a):
        op("V", lambda: V.transpose(out["ap"], a["ap"]), [out], [a], wide(a))

    def quant(q, s, x):
        op("V", lambda: V.quantize_mx(q["ap"], s["ap"], x["ap"]), [q, s], [x], 0.012 + wide(x, 0.265))

    def act(out, a, f=AF.Copy, scale=None, bias=None, acc=None):
        kw, ins, outs = {}, [a], [out]
        if scale is not None:
            kw["scale"] = scale
        if bias is not None:
            kw["bias"] = bias["ap"]
            ins.append(bias)
        if acc is not None:
            kw["accum_out"] = acc["ap"]
            outs.append(acc)
        op("S", lambda: S.activation(out["ap"], a["ap"], f, **kw), outs, ins, 0.065 + wide(out, 1.5 if a["aux"] else 1.0))

    def mm(out, l, ls, r, rs):
        op("T", lambda: TE.matmul_mx(out["ap"], l["ap"], ls["ap"], r["ap"], rs["ap"], True, True), [out], [l, ls, r, rs], 0.02 + wide(r))

    def dma(q, sem, out, in_):
        op(q, lambda: eng[q].dma_start(out["ap"], in_["ap"]), [out], [in_], 0.07, sem=sem, lat=2.0)

    def iota(out, pat, cm):
        kw = {} if out["reg"][0] in ("pi", "s2", "s8") else {"allow_small_or_imprecise_dtypes": True}
        op("G", lambda: g.iota(out["ap"], pat, 0, cm, **kw), [out], [], 0.13 + wide(out, 2))

    def send(dst, out, src, sem):
        return op("G", lambda: put(g, T, topo, core, dst, out["ap"], src["ap"], sem), [], [src], 0.1, sem="snt", val=8)

    def fold(out, n_out, src, n, mask):
        tt(W("fa", 0, n), src, W(mask, 0, n), A.mult)
        a, b = "fa", "fb"
        while n > n_out:
            n //= 2
            tt(out if n == n_out else W(b, 0, n), W(a, 0, 2 * n, 2), W(a, 1, 2 * n, 2), A.add)
            a, b = b, a

    def blk(p):
        return p // 2 + 4 * (p % 2)

    relA, relB = relays(topo, T.cores, rank)

    dma("Y", "dX", W("xt", 0, 1024), ext(T.x[:, :]))
    dma("S", "dU", W("ut", 0, 512), ext(T.u[:, :]))
    for k in range(8):
        t = (0, 4, 2, 6, 1, 5, 3, 7)[k]
        dma("Y" if k % 2 else "S", "dN", W("nbi", 2 * k, 2 * k + 2), ext(T.nb[16 * t:16 * t + 16, :]))
    fill(W("pin", 0, 32), 0)
    for a in range(8):
        q, h = a // 2, a % 2
        dma("Y" if h else "S", "dP", W("pin", 16 * h, 16 * h + 13, 1, 32 * q, 32 * q + 32), ext(T.p[16 * a:16 * a + 16, :]))
    dma("Y", "dW", u8(W("wq", 0, 512)), ext(T.wc[:, :]))
    dma("Y", "dW", W("wqs", 0, 512), ext(T.ws[:, :]))
    dma("Y", "dV", W("vt", 0, 512), ext(T.v[:, :]))

    iota(W("pi", 0, 1), [[0, 1]], 1)
    iota(W("s8", 0, 8), [[0, 8]], 1)
    iota(W("s2", 0, 2), [[1, 2]], 2)
    iota(W("ic", 0, 256), [[1, 256]], 0)
    iota(W("encs", 0, 256), [[1, 16], [16, 16]], 0)
    iota(W("pl0", 0, 32), [[0, 2], [16, 16]], 0)
    fill(W("ones", 0, 512), 1.0)
    for b in range(4):
        o, i = W("eb", 512 * b, 512 * b + 512), W("ones", 0, 512)
        op("G", lambda o=o, i=i, b=b: g.affine_select(o["ap"], i["ap"], [[-1, 512]], A.is_equal, 0.0, b, 4), [o], [i], 1.0)
    iota(W("m16", 0, 256), [[0, 16], [1, 16]], 0)
    iota(W("wcs", 0, 16), [[16, 16]], 0)
    iota(W("i96", 0, 96), [[1, 96]], 0)
    ts(W("s8", 0, 8), W("s8", 0, 8), 7, A.bitwise_and)
    ts(W("lu", 0, 8), W("s8", 0, 8), 16, A.mult)
    ts(W("nsi", 0, 8), W("s8", 0, 8), 1, A.bitwise_and)
    ts(W("lb", 0, 8), W("nsi", 0, 8), 112, A.mult)
    quant(W("qu", 0, 128), W("qus", 0, 128), W("ut", 0, 512))
    for q, s, l in (("bq", "bqs", "lb"), ("uq", "uqs", "lu")):
        cp(u32(W(q, 0, 128)), ind(u32(W("qu", 0, 128)), W(l, 0, 8)))
        cp(W(s, 0, 128), ind(W("qus", 0, 128), W(l, 0, 8)))
    quant(W("qc0", 0, 256), W("qs0", 0, 256), W("xt", 0, 1024))
    ts(W("nsi", 0, 1), W("pi", 0, 1), 15, A.bitwise_and)
    cp(W("cst", 0, 1), W("nsi", 0, 1))
    lane = W("cst", 0, 1)
    ts(W("cst", 1, 2), lane, 8, A.is_equal)
    ts(W("cst", 2, 3), lane, 9, A.is_equal)
    tt(W("cst", 3, 4), W("cst", 1, 2), W("cst", 2, 3), A.add)
    ts(W("cst", 4, 5), W("cst", 3, 4), LOW, A.mult, LOW, A.subtract)
    ts(W("enc", 0, 256), W("ic", 0, 256), UNIT, A.mult, BIGID, A.add)
    ts(W("encs", 0, 256), W("encs", 0, 256), UNIT, A.mult, BIGID, A.add)
    ts(W("cmax", 0, 256), W("enc", 0, 256), W("cst", 1, 2), A.mult, W("cst", 4, 5), A.add)
    ts(W("encs", 0, 256), W("encs", 0, 256), W("cst", 2, 3), A.mult)
    tt(W("cmax", 0, 256), W("cmax", 0, 256), W("encs", 0, 256), A.add)
    ts(W("s2", 0, 2), W("s2", 0, 2), 15, A.bitwise_and)
    ts(W("nsi", 2, 3), W("pi", 0, 1), 3, A.arith_shift_right)
    cp(W("cst", 5, 6), W("nsi", 2, 3))
    ts(W("nbl", 16, 18), W("s2", 0, 2), 16, A.mult, W("cst", 5, 6), A.add)
    cp(W("nbl", 0, 16), W("nbi", 0, 16))
    cp(W("nbv", 0, 288), ind(W("enc", 0, 256), W("nbl", 0, 18)))
    tt(W("d1", 0, 128), W("nbv", 128, 256), W("nbv", 0, 128), A.subtract)
    ts(W("nsi", 3, 4), W("pi", 0, 1), 1, A.bitwise_and)
    ts(W("nsi", 4, 5), W("pi", 0, 1), 31, A.bitwise_and)
    ts(W("nsi", 5, 6), W("nsi", 4, 5), 1, A.arith_shift_right)
    ts(W("cst", 6, 7), W("nsi", 3, 4), 208, A.mult)
    tt(W("cst", 7, 8), W("cst", 6, 7), W("nsi", 5, 6), A.add)
    ts(W("pl0", 0, 32), W("pl0", 0, 32), W("cst", 7, 8), A.add)
    ts(W("cz", 0, 32), W("pin", 0, 32), 1024, A.mult)
    tt(W("cz", 0, 32), W("cz", 0, 32), W("pl0", 0, 32), A.add)

    def to_chains():
        for a in range(8):
            q, h = a // 2, a % 2
            dma("Y", "dZ", W("zc", 4 * blk(a), 4 * blk(a) + 4), W("cz", 16 * h, 16 * h + 16, 1, 32 * q, 32 * q + 32))
    to_chains()
    fill(W("jt", 0, 256), 0.0)
    fill(W("fl0", 0, 64), 1.0)
    fill(W("fl1", 0, 64), 1.0)
    fill(W("at", 384, 512), 0.0)
    for t in range(R):
        fill(W("lo%d" % t, 0, 8), 0)
    CW, CI, CWM, B10, B17 = [lambda k=0, n=16, o=o: W("wcs", o + k, o + k + n) for o in (0, 16, 32, 48, 64)]
    quant(W("qe", 0, 512), W("qes", 0, 512), W("eb", 0, 2048))
    ts(W("fm", 0, 256), W("m16", 0, 256), lane, A.is_equal)
    ts(W("a1k", 0, 256), W("ic", 0, 256), 1024.0, A.mult)
    ts(W("fm2", 0, 256), W("fm", 0, 256), 2.0 ** -8, A.mult)
    ts(W("b256", 0, 256), W("ic", 0, 256), 256.0, A.mult)
    ts(CW(), CW(), lane, A.add)
    ts(W("a17", 0, 256), W("ic", 0, 256), 2.0 ** 17, A.mult)
    cp(W("sbw", 416, 672), W("b256", 0, 256))
    ts(CI(), CW(), 416.0, A.add)
    ts(CWM(), CW(), 256.0, A.subtract)
    ts(B10(), CW(), -1024.0, A.mult)
    ts(B17(), CW(), -2.0 ** 17, A.mult, 2.0 ** 24, A.add)
    ts(W("i96", 0, 96), W("i96", 0, 96), 2.0 ** 24, A.subtract)
    quant(W("qv", 0, 128), W("qvs", 0, 128), W("vt", 0, 512))

    def code(out, x):
        ts(out, x, 1 / UNIT, A.mult, 256.0, A.subtract)

    def half_step(n):
        tn, nt, no = "t%d" % (n % 2), "t%d" % ((n + 1) % 2), "o%d" % ((n + 1) % 2)
        nx = "l%d" % ((n + 1) % 2)
        par = (n - 1) % 2
        fl = "fl%d" % par
        ids = lambda b0, b1: W(tn, 64 * b0 + 8, 64 * b1, 16)
        sc = lambda b, t: W(tn, 64 * b + t, 64 * b + 64, 16)
        stay, move = 16 - 16 * par, 16 * par
        if n < 4:
            code(W(nx, stay, stay + 16), ids(4 - 4 * par, 8 - 4 * par))
            pv = blk(7 - 7 * par)
            code(W(nx, 32, 36), W(tn, 64 * pv + 9, 64 * pv + 64, 16))
            act(W(no, 16 * stay, 16 * stay + 256), ind(W("tab", 0, 256), W(nx, stay, stay + 16)))
            act(W(no, 512, 576), ind(W("jt", 0, 256), W(nx, 32, 36)))
        else:
            code(W("fi", 0, 16), ids(0, 4))
        GL, GH, HI, LO = 0, 16, 32, 48
        PW, DD, MM, SN, NI = [W("sm", o, o + k) for o, k in ((0, 32), (32, 32), (64, 32), (96, 16), (112, 16))]
        D = lambda a, b: W("sm", 32 + a, 32 + b)
        for i in range(4):
            s, o = (2 * i, 4 + i) if par == 0 else (2 * i + 1, i)
            f = (GH if par == 0 else GL) + 4 * i
            tt(W(fl, f, f + 4), sc(o, s), sc(4 * par + i, s), A.is_gt)
        for i in range(3):
            s, o, m = (2 * i + 2, 4 + i, i + 1) if par == 0 else (2 * i + 1, i + 1, 4 + i)
            f = GL + 4 * i + 4 if par == 0 else GH + 4 * i
            tt(W(fl, f, f + 4), sc(o, s), sc(m, s), A.is_gt)
        if par == 0:
            tt(W(fl, HI, HI + 16), ids(0, 4), ids(4, 8), A.is_equal)
            tt(W(fl, LO + 4, LO + 16), ids(1, 4), ids(4, 7), A.is_equal)
            tt(D(16, 32), ids(4, 8), ids(0, 4), A.subtract)
            tt(D(4, 16), ids(4, 7), ids(1, 4), A.subtract)
            tt(PW, W(fl, 0, 32), W(fl, 32, 64), A.mult)
            tt(D(0, 4), W(tn, 512, 576, 16), ids(0, 1), A.subtract)
        else:
            tt(W(fl, LO, LO + 16), ids(0, 4), ids(4, 8), A.is_equal)
            tt(W(fl, HI, HI + 12), ids(4, 7), ids(1, 4), A.is_equal)
            tt(D(0, 16), ids(0, 4), ids(4, 8), A.subtract)
            tt(D(16, 28), ids(1, 4), ids(4, 7), A.subtract)
            tt(PW, W(fl, 0, 32), W(fl, 32, 64), A.mult)
            tt(D(28, 32), W(tn, 520, 576, 16), ids(7, 8), A.subtract)
        tt(MM, PW, DD, A.mult)
        tt(SN, W("sm", 64, 80), W("sm", 80, 96), A.add)
        tt(NI, SN, ids(4 * par, 4 * par + 4), A.add)
        if n == 4:
            code(W("fi", 16, 32), NI)
            return
        code(W(nx, move, move + 16), NI)
        hi, lo = 16 * move, 16 * stay
        act(W(no, hi + 128, hi + 256), ind(W("tab", 0, 256), W(nx, move + 8, move + 16)))
        cp(W(no, hi, hi + 128), ind(W("tab", 0, 256), W(nx, move, move + 8)))
        tr(W(nt, lo, lo + 256), W(no, lo, lo + 256))
        tr(W(nt, 512, 576), W(no, 512, 576))
        tr(W(nt, hi, hi + 256), W(no, hi, hi + 256))

    def next_chains():
        tt(W("z1s", 0, 96), ind(W("a1k", 0, 256), W("laa", 0, 6)), W("pii", 0, 96), A.add)

    for r in range(R):
        q, s, lo, la = "qc%d" % r, "qs%d" % r, "lo%d" % r, "la%d" % r
        if r:
            quant(W(q, 0, 256), W(s, 0, 256), W("mt", 0, 1024))
        s1 = send(relA, u8(W("rc%d" % r, 0, 256)), u8(W(q, 0, 256)), "aC%d" % r)
        s2 = send(relB, W("rs%d" % r, 0, 256), W(s, 0, 256), "aS%d" % r)
        if r == 0:
            iota(W("id1", 0, 4096), [[1, 4096]], 0)
        mq, ms = W(q, 0, 256), W(s, 0, 256)
        mm(W("pb", 512, 768), W("bq", 0, 128), W("bqs", 0, 128), mq, ms)
        mm(W("pb", 0, 256), W("uq", 0, 128), W("uqs", 0, 128), mq, ms)
        if r:
            next_chains()
            tr(W("zt", 0, 416), W("z1s", 0, 416))
            for h in range(2):
                cp(W("cz", 16 * h, 16 * h + 13), W("zt", 16 * h, 416, 32))
            to_chains()
        act(W("bt", 0, 256), W("pb", 512, 768))
        act(W("ns", 0, 288), ind(W("bt", 0, 256), W("nbl", 0, 18)))
        tt(W("tab", 0, 256), W("pb", 0, 256), W("cmax", 0, 256), A.max)
        tw, ti, ns = [lambda a, b, k=k: W(k, a, b) for k in ("tw", "ti", "ns")]
        tt(tw(128, 256), ns(0, 128), ns(128, 256), A.max)
        tt(tw(0, 128), ns(128, 256), ns(0, 128), A.is_gt)
        tt(tw(320, 384), tw(128, 192), tw(192, 256), A.max)
        tt(ti(0, 128), tw(0, 128), W("d1", 0, 128), A.mult)
        tt(tw(256, 320), tw(192, 256), tw(128, 192), A.is_gt)
        tt(ti(128, 256), ti(0, 128), W("nbv", 0, 128), A.add)
        tt(tw(416, 448), tw(320, 352), tw(352, 384), A.max)
        tt(ti(256, 320), ti(192, 256), ti(128, 192), A.subtract)
        tt(tw(384, 416), tw(352, 384), tw(320, 352), A.is_gt)
        tt(ti(320, 384), ti(256, 320), tw(256, 320), A.mult)
        tt(tw(448, 480), tw(416, 448), ns(256, 288), A.is_gt)
        tt(ti(384, 448), ti(320, 384), ti(128, 192), A.add)
        tt(ti(448, 480), ti(416, 448), ti(384, 416), A.subtract)
        tt(ti(480, 512), ti(448, 480), tw(384, 416), A.mult)
        tt(ti(0, 32), ti(480, 512), ti(384, 416), A.add)
        tt(ti(32, 64), ti(0, 32), W("nbv", 256, 288), A.subtract)
        tt(ti(64, 96), ti(32, 64), tw(448, 480), A.mult)
        tt(W("jb", 0, 32, 2), ti(64, 80), W("nbv", 256, 272), A.add)
        tt(W("jb", 1, 32, 2), ti(80, 96), W("nbv", 272, 288), A.add)
        for h in range(8):
            dma("Y" if h % 2 else "S", "dJ", W("jt", 32 * h, 32 * h + 32, 1, 0, 128, 8), W("jb", 0, 32, 1, 16 * h, 16 * h + 16))
        ts(W("ids", 0, 32), W("zc", 0, 32), 10, A.arith_shift_right)
        cp(W("l1", 0, 32), W("ids", 0, 32))
        act(W("o1", 256, 512), ind(W("tab", 0, 256), W("l1", 16, 32)))
        cp(W("o1", 0, 256), ind(W("tab", 0, 256), W("l1", 0, 16)))
        ts(W("sw4", 0, 4), W("ids", 0, 4), 15, A.bitwise_and)
        ts(W("sw4", 8, 12), W("ids", 0, 4), 4, A.arith_shift_right)
        ts(W("sw4", 4, 8), W("sw4", 0, 4), 16, A.mult)
        tt(W("sw4", 12, 16), W("sw4", 4, 8), W("sw4", 8, 12), A.add)
        cp(W("l1", 32, 36), W("sw4", 12, 16))
        ts(W("pl", 0, 4), W("zc", 0, 4), 1023, A.bitwise_and)
        tr(W("t1", 0, 256), W("o1", 0, 256))
        tr(W("t1", 256, 512), W("o1", 256, 512))
        qe = lambda b: (W("qe", 128 * b, 128 * b + 128), W("qes", 128 * b, 128 * b + 128))
        for b in range(4):
            mm(W("pa", 512 * b, 512 * b + 256), qe(b)[0], qe(b)[1], mq, ms)
        for b in range(4):
            act(W("fh", 256 * b, 256 * b + 256), W("pa", 512 * b, 512 * b + 256), scale=0.5)
        act(W("o1", 512, 576), ind(W("jt", 0, 256), W("l1", 32, 36)))
        tr(W("t1", 512, 576), W("o1", 512, 576))
        for n in range(1, 5):
            half_step(n)
        fi, eq, k4 = [lambda a, b, k=k: W(k, a, b) for k in ("fi", "eq", "k4")]
        tt(eq(0, 16), fi(0, 16), fi(16, 32), A.is_equal)
        tt(eq(16, 28), fi(16, 28), fi(4, 16), A.is_equal)
        ts(fi(32, 64), fi(0, 32), 256.0, A.mult)
        tt(eq(32, 44), eq(0, 12), eq(16, 28), A.add)
        tt(W("ob", 0, 32, 2), fi(0, 16), fi(48, 64), A.add)
        tt(eq(44, 48), eq(32, 36), eq(36, 40), A.add)
        tt(eq(48, 52), eq(40, 44), eq(12, 16), A.add)
        tt(W("ob", 32, 56, 2), fi(16, 28), fi(36, 48), A.add)
        tt(eq(52, 56), eq(44, 48), eq(48, 52), A.add)
        tt(W("ob", 56, 64, 2), fi(28, 32), fi(44, 48), A.add)
        ts(eq(56, 60), eq(52, 56), 512.0, A.mult)
        tt(k4(0, 4), eq(56, 60), W("pl", 0, 4), A.add)
        for a in range(8):
            cp(W("ob", 8 * a + 1, 8 * a + 8, 2), k4(0, 4))
        for a in range(8):
            dma("Y" if a % 2 else "S", "dK", W("gb", 0, 64, 1, 16 * a, 16 * a + 16), W("ob", 8 * blk(a), 8 * blk(a) + 8))
        ts(k4(4, 8), k4(0, 4), -1.0, A.mult)
        ts(W("fq", 0, 1024), W("fh", 0, 1024), 0.5, A.mult)
        ts(W("fr", 0, 1024), W("fh", 0, 1024), 0.5, A.mult)
        cp(W("gk", 0, 32), W("gb", 1, 64, 2))
        act(W("kr", 208, 416), ind(W("id1", 0, 4096), W("gk", 16, 29)))
        cp(W("kr", 0, 208), ind(W("id1", 0, 4096), W("gk", 0, 13)))
        for i in range(1, 4):
            act(W("dum", 416 * i - 416, 416 * i), W("kr", 0, 416), AF.Sign, bias=k4(4 + i, 5 + i), acc=k4(8 + i, 9 + i))
        ts(W("cmp", 0, 416), W("kr", 0, 416), k4(0, 1), A.is_lt)
        red(k4(8, 9), W("cmp", 0, 416), A.add)
        cp(W("rk", 0, 1), k4(8, 9))
        ts(W("iab", 0, 32), W("gb", 0, 64, 2), 255, A.bitwise_and)
        ts(W("iab", 32, 64), W("gb", 0, 64, 2), 8, A.arith_shift_right)
        ts(W("iab", 64, 96), W("gb", 1, 64, 2), 511, A.bitwise_and)
        ts(W("rk", 1, 4), k4(9, 12), -0.5, A.mult, 207.5, A.add)
        for a in range(8):
            dma("Y" if a % 2 else "S", "dR", W("gr", 0, 32, 1, 16 * a, 16 * a + 16), W("rk", 0, 4))
        cp(W("lsb", 0, 32), W("iab", 32, 64))
        cp(W("lsa", 0, 32), W("iab", 0, 32))
        cp(W("lsp", 0, 32), W("iab", 64, 96))
        for c0, c1, e0, e1 in HALF:
            act(W("br", e0, e1), ind(W("b256", 0, 256), W("lsb", c0, c1)))
            cp(W("ar", e0, e1), ind(W("ic", 0, 256), W("lsa", c0, c1)))
        tt(W("z2r", 0, 416), W("ar", 0, 416), W("br", 0, 416), A.add)
        act(W("z1r", 0, 416), W("ar", 0, 416), scale=1024.0)
        for c0, c1, e0, e1 in HALF:
            act(W("plr", e0, e1), ind(W("id1", 0, 512), W("lsp", c0, c1)))
        cp(W("lr", 0, 32), W("gr", 0, 32))
        for c0, c1, e0, e1 in HALF:
            cp(ind(W("z2s", 0, 416), W("lr", c0, c1)), W("z2r", e0, e1))
        fold(W(lo, 0, 6), 6, W("z2s", 0, 96), 96, "fm")
        s3 = send(relB, W("rl%d" % r, 0, 8), W(lo, 0, 8), "aL%d" % r)
        landed("fc%d" % r, 256, "bC%d" % r, s1)
        landed("fs%d" % r, 256, "bS%d" % r, s2)
        for b in range(4):
            mm(W("pb", 512 * b, 512 * b + 256), qe(b)[0], qe(b)[1], W("fc%d" % r, 0, 256), W("fs%d" % r, 0, 256))
        tt(W("z1r", 0, 416), W("z1r", 0, 416), W("plr", 0, 416), A.add)
        for c0, c1, e0, e1 in HALF:
            cp(ind(W("z1s", 0, 416), W("lr", c0, c1)), W("z1r", e0, e1))
        for c0, c1, e0, e1 in HALF:
            cp(ind(W("sbw", 0, 416), W("lsp", c0, c1)), W("br", e0, e1))
        cp(W("zi", 0, 96), W("z1s", 0, 96))
        ts(W("pii", 0, 96), W("zi", 0, 96), 1023, A.bitwise_and)
        ts(W("py", 0, 96), W("pii", 0, 96), 128.0, A.mult)
        tt(W("py", 0, 96), W("py", 0, 96), W("i96", 0, 96), A.add)
        for k in range(16):
            o = 320 * (k % 8)
            act(W("ab", o, o + 320), W("z1s", 96, 416), AF.Abs, bias=B10(k, 1))
            low2(W("sco", 160 * k, 160 * k + 160), W("ab", o, o + 160), W("ab", o + 160, o + 320))
        for b in range(4):
            act(W("fp", 256 * b, 256 * b + 256), W("pb", 512 * b, 512 * b + 256), scale=0.5)
        lt, lf = [lambda a, b, k=k: W(k, a, b) for k in ("lt", "lf")]
        low, lowa = W("sco", 159, 2560, 160), W("sca", 47, 768, 48)
        ts(lt(0, 16), low, 415.5, A.is_gt)
        tt(lt(16, 32), CI(), low, A.subtract)
        tt(lt(32, 48), lt(0, 16), lt(16, 32), A.mult)
        tt(lt(48, 64), lt(32, 48), low, A.add)
        cp(W("lsl", 0, 16), lt(48, 64))
        cp(W("brr", 0, 256), ind(W("sbw", 0, 672), W("lsl", 0, 16)))
        fold(lt(0, 16), 16, W("brr", 0, 256), 256, "fm2")
        cp(W("lbl", 0, 16), lt(0, 16))
        for b in range(4):
            tt(W("hl", 352 * b, 352 * b + 256), ind(W("fq", 256 * b, 256 * b + 256), W("lbl", 0, 16)), W("fr", 256 * b, 256 * b + 256), A.add)
        landed(la, 8, "bL%d" % r, s3)
        ts(W("ia", 8, 16), W(la, 0, 8), 8, A.arith_shift_right)
        ts(W("ia", 0, 8), W(la, 0, 8), 255, A.bitwise_and)
        cp(W("lbb", 0, 8), W("ia", 8, 16))
        cp(W("laa", 0, 8), W("ia", 0, 8))
        fp = lambda b, l: ind(W("fp", 256 * b, 256 * b + 256), W(l, 0, 6))
        for b in range(4):
            act(W("tb", 96 * b, 96 * b + 96), fp(b, "lbb"))
        tt(W("zy", 0, 96), ind(W("a17", 0, 256), W("laa", 0, 6)), W("py", 0, 96), A.add)
        for b in range(4):
            tt(W("at", b, 384, 4), fp(b, "laa"), W("tb", 96 * b, 96 * b + 96), A.add)
        quant(W("qa", 0, 128), W("qas", 0, 128), W("at", 0, 512))
        for b in range(4):
            mm(W("pa", 512 * b, 512 * b + 128), W("wq", 128 * b, 128 * b + 128), W("wqs", 128 * b, 128 * b + 128), W("qa", 0, 128), W("qas", 0, 128))
        for k in range(16):
            o = 96 * (k % 8)
            act(W("aa", o, o + 96), W("zy", 0, 96), AF.Abs, bias=B17(k, 1))
            low2(W("sca", 48 * k, 48 * k + 48), W("aa", o, o + 48), W("aa", o + 48, o + 96))
        for b in range(4):
            act(W("hl", 352 * b + 256, 352 * b + 352), W("pa", 512 * b, 512 * b + 96), scale=2.0 ** -6)
        ts(lf(0, 16), low, 128.0, A.mult, 60000.0, A.min)
        cp(W("lai", 0, 16), lowa)
        tt(lf(16, 32), lowa, lf(0, 16), A.is_lt)
        ts(W("lai", 16, 32), W("lai", 0, 16), 127, A.bitwise_and)
        tt(lf(32, 48), W("lai", 16, 32), CWM(), A.subtract)
        tt(lf(48, 64), lf(32, 48), lf(16, 32), A.mult)
        tt(lt(0, 16), lf(48, 64), CW(), A.add)
        cp(W("lfl", 0, 16), lt(0, 16))
        for b in range(4):
            tt(W("mt", b, 1024, 4), ind(W("hl", 352 * b, 352 * b + 352), W("lfl", 0, 16)), W("fh", 256 * b, 256 * b + 256), A.add)
    quant(W("qc3", 0, 256), W("qs3", 0, 256), W("mt", 0, 1024))
    dma("Y", "dO", ext(T.oc[:, :]), u8(W("qc3", 0, 256)))
    for k in range(4):
        dma("Y", "dO", ext(T.osc[4 * k:4 * k + 4, :]), W("qs3", 0, 256, 1, 32 * k, 32 * k + 4))
    mm(W("pa", 0, 256), W("qv", 0, 128), W("qvs", 0, 128), W("qc3", 0, 256), W("qs3", 0, 256))
    act(W("yo", 0, 256), W("pa", 0, 256))
    dma("S", "dO", ext(T.y[:, :]), W("yo", 0, 256))
    next_chains()
    for c0, c1, e0, e1 in HALF:
        cp(W("ar", e0, e1), ind(W("z1s", 0, 416), W("lr", c0, c1)))
    for c0, c1, e0, e1 in HALF:
        cp(ind(W("br", 0, 416), W("lsp", c0, c1)), W("ar", e0, e1))
    cp(W("kri", 0, 416), W("br", 0, 416))
    ts(W("kri", 0, 416), W("kri", 0, 416), 10, A.arith_shift_right)
    cp(W("ado", 0, 416), W("kri", 0, 416))
    dma("Y", "dO", ext(T.ad[:, :]), W("ado", 0, 416, 1, 0, 128, 16))
    issue()
